import numpy as np, ml_dtypes
CORES = [5,29,101,125,133,157,229,253]
N = 8
import mx_ref
BF = ml_dtypes.bfloat16
def entries(a):
    return np.ascontiguousarray(a.T).reshape(-1)
def table(e):
    return np.ascontiguousarray(np.reshape(e, (-1, 16)).T).astype(np.int32)
def cols(t, e):
    v = np.concatenate([t.reshape(128, -1, 4), np.zeros((128, 1, 4), BF)], axis=1)
    return np.ascontiguousarray(v[:, e]).reshape(128, -1)
def cut(t, i, w=512):
    return t[:, w * i:w * i + w]
def f(rng, *shape):
    return mx_ref.flush((rng.standard_normal(shape, dtype=np.float32) * np.exp2(rng.integers(-2, 3, shape[:-1] + (1,)))).astype(BF))
def wide(rng, *shape, cols=0):
    v = rng.standard_normal(shape, dtype=np.float32) * np.exp2(rng.integers(-12, 13, shape)).astype(np.float32)
    if cols: v *= np.repeat(np.exp2(rng.integers(-cols, cols + 1, shape[:-2] + (1, shape[-1] // 4))) * (rng.random(shape[:-2] + (1, shape[-1] // 4)) > 0.0625), 4, axis=-1).astype(np.float32)
    return mx_ref.flush(v.astype(BF))
C, P, B, O, DN, DS = 128, 256, 2, 2, 160, 80
def lists(rng, S, straddle=0.5, fill="any", flip=None):
    o = np.array([[max(0, min(S[r + 1], P * q + P) - max(S[r], P * q)) for q in range(N)] for r in range(N)])
    ends, both = np.zeros((N, N), int), {}
    for r in range(N):
        for q in range(N - 1):
            if o[r, q] > 0 and o[r, q + 1] > 0 and rng.random() < straddle:
                a = int(rng.integers(1, min(5, o[r, q]) + 1))
                b = int(rng.integers(1, min(6 - a, o[r, q + 1]) + 1))
                if fill == "few":
                    a = int(o[r, q] % 6); b = 6 - a
                    if a == 0: continue
                o[r, q] -= a; o[r, q + 1] -= b
                ends[r, q] += 1; ends[r, q + 1] += 1; both[r, q] = a + b
    K = np.floor_divide(o + 5, 6)
    segs = [(r, q) for r in range(N) for q in range(N) if o[r, q] > 0]
    segs = [segs[i] for i in rng.permutation(len(segs))]
    if fill == "full": segs = [s for s in segs if s[1] % 2 == 1] + [s for s in segs if s[1] % 2 == 0]
    if fill == "few": segs = []
    for r, q in segs:
        room = int(min(DS - ends[r, q] - K[r, q], o[r, q] - K[r, q], C - (ends[r].sum() >> 1) - K[r].sum(), DN - ends[:, q].sum() - K[:, q].sum()))
        K[r, q] += room if fill == "full" else rng.integers(0, room + 1)
    m = np.zeros((N, C), int)
    for r in range(N):
        e = []
        for q in range(N):
            k = int(K[r, q])
            e += (1 + np.bincount(rng.permutation(np.repeat(np.arange(k), 5))[:o[r, q] - k], minlength=k)).tolist()
            if (r, q) in both: e.append(both[r, q])
        m[r, np.sort(rng.permutation(C)[:len(e)])] = np.array(e, int)
    if flip is None: flip = rng.random() < 0.5
    if flip: m = m[::-1, ::-1]
    return {"cnt": np.stack([table(e) for e in m])}
def begins(rng):
    for k in range(50):
        S, e = [0], 1 - 2 * int(rng.integers(2))
        turn = N if rng.random() < 0.5 else int(rng.integers(2, N))
        for r in range(1, N):
            if r == turn: e = -e
            s = S[-1] - P * (r - 1)
            lo = max(s - P, -2 * P, -((3 * P * (N - r)) >> 1))
            hi = min(s + ((3 * P) >> 1), 2 * P, P * (N - r))
            a, b = (max(lo, (3 * P) >> 2), hi) if e > 0 else (lo, min(hi, -((3 * P) >> 2)))
            if a > b: a = b = hi if e > 0 else lo
            S.append(P * r + int(rng.integers(a, b + 1)))
        S.append(N * P)
        own = sum(max(0, min(S[r + 1], P * r + P) - max(S[r], P * r)) for r in range(N))
        if 2 * own <= N * P: return S
    raise RuntimeError("begins")
def floats(rng):
    return {"x": f(rng, N, 128, 4 * C), "w": f(rng, N, 128, 512 * B * O)}
def setup_inputs(rng):
    return {**floats(rng), **lists(rng, begins(rng))}
def setup_inputs_full(rng):
    S = [0] + [P * r + (P >> 1) + int(rng.integers(-(P >> 4), (P >> 4) + 1)) for r in range(1, N)] + [N * P]
    return {**floats(rng), **lists(rng, S, straddle=2.0, fill="full")}
def setup_inputs_furthest(rng):
    S = [0] + [min(P * (r + 2), N * P) for r in range(1, N + 1)]
    return {**floats(rng), **lists(rng, S, straddle=2.0, fill="few")}
def setup_inputs_dense(rng):
    def some(k, n):
        return (1 + np.bincount(rng.permutation(np.repeat(np.arange(k), 5))[:n - k], minlength=k)).tolist()
    H = min(P // 256 * 128 + 64, P - DS) if N > 4 else (P - 1) // 256 * 128 + 64
    X = (7 * DS - P) // 5
    flip = bool(rng.random() < 0.5)
    front = 3 + 2 * int(rng.integers((N - 2) // 2))
    e = [[] for r in range(N)]
    for q in range(2, N):
        h, i, j = P // 2, 0, 0
        if q == front: h, i, j = (P - DS, X, DS) if flip else (DS, DS, X)
        elif q % 2 == 1 or N == 4: h, i, j = H, H % 128, 128 - H % 128
        a, b = h - i, P - h - j
        if q == 2: a += 2 * P
        if q % 2 == 1: ka, kb = DS - i, DS - j
        else:
            ka = int(rng.integers(-(-a // 6), (C if q == 2 else C - DS) - i + 1))
            kb = int(rng.integers(-(-b // 6), C - DS - j + 1))
        e[q - 2] += some(ka, a) + [1] * i
        e[q - 1] += [1] * j + some(kb, b)
    m = np.zeros((N, C), int)
    for r in range(N):
        m[r, np.sort(rng.permutation(C)[:len(e[r])])] = np.array(e[r], int)
    if flip: m = m[::-1, ::-1]
    return {**floats(rng), "cnt": np.stack([table(v) for v in m])}
def setup_inputs_many(rng):
    def some(k, n):
        return (1 + np.bincount(rng.permutation(np.repeat(np.arange(k), 5))[:n - k], minlength=k)).tolist()
    src = [[0], [0, 1, 2, 3], [3], [3]] if N == 4 else [[0], [0], [0, 1, 2, 3, 4], [4], [4], [4, 5, 6, 7], [7], [7]]
    flip = bool(rng.random() < 0.5)
    lo = -(-P // 6)
    alone = [src.count([r]) for r in range(N)]
    among = [sum(len(s) > 1 and r in s for s in src) for r in range(N)]
    least = [alone[r] * lo + (1 - among[r] - alone[r] * lo) % N for r in range(N)]
    k = np.zeros((N, N), int)
    for q, s in enumerate(src):
        if len(s) == 1: continue
        c = np.ones(len(s), int)
        c[int(rng.integers(1, len(s) - 1))] = N - len(s) + 1
        top = np.array([(min(DS, (C - least[r]) // among[r]) - int(c[i])) // N for i, r in enumerate(s)])
        j = np.ones(len(s), int)
        while j.sum() < DN // N - 1: j[int(rng.choice(np.flatnonzero(j < top)))] += 1
        k[s, q] = N * j + c
    for r in range(N):
        n = alone[r]
        if n == 0: continue
        z = min(C - int(k[r].sum()), n * DS)
        w = least[r] + N * int(rng.integers(0, (z - least[r]) // N + 1))
        for q in range(N):
            if src[q] == [r]:
                n -= 1
                u = int(rng.integers(max(lo, w - DS * n), min(DS, w - lo * n) + 1))
                k[r, q] = u; w -= u
    e = [[] for r in range(N)]
    for q, s in enumerate(src):
        v = some(int(k[:, q].sum()), P)
        for r in s:
            i = int(k[r, q])
            e[r] += v[:i]; v = v[i:]
    m = np.zeros((N, C), int)
    for r in range(N):
        m[r, np.sort(rng.permutation(C)[:len(e[r])])] = np.array(e[r], int)
    if flip: m = m[::-1, ::-1]
    return {**floats(rng), "cnt": np.stack([table(v) for v in m])}
def setup_inputs_spread(rng):
    d = setup_inputs(rng); v = np.array(wide(rng, N, 128, 4 * C, cols=6))
    v[np.abs(v.astype(np.float32)) < 2.0 ** -30] = 0
    d["x"] = v; return d
def check_inputs(d):
    b = []
    for k in ("x", "w"):
        v = np.abs(d[k].astype(np.float32))
        if not ((v == 0) | ((v >= 2.0 ** -30) & (v <= 2.0 ** 30))).all(): b.append("the range of " + k)
    m = np.stack([entries(a) for a in d["cnt"]])
    if m.min() < 0 or m.max() > 6: return b + ["cnt"]
    if m.sum() != N * P: return b + ["the sum of all counts"]
    runs = np.repeat(np.arange(N * C), m.reshape(-1)).reshape(N, P)
    for q in range(N):
        u = np.unique(runs[q])
        k = np.bincount(np.floor_divide(u, C), minlength=N)
        if len(u) > DN: b.append("different columns in a run")
        if k.max() > DS: b.append("different columns of one rank in a run")
        if (np.abs(np.flatnonzero(k) - q) > 2).any(): b.append("a column of a rank more than two away")
    return b
def reference(x, w, cnt):
    m = np.stack([entries(a) for a in cnt])
    runs = np.repeat(np.arange(N * C), m.reshape(-1)).reshape(N, P)
    t = np.concatenate([x[r] for r in range(N)], axis=1)
    y = np.zeros((N, 128, O * P), np.float32)
    for q in range(N):
        for b in range(B):
            c = mx_ref.quantize(cols(t, runs[q, 128 * b:128 * b + 128]))
            for o in range(O):
                i = P * o + 128 * b
                y[q][:, i:i + 128] = mx_ref.matmul(mx_ref.quantize(cut(w[q], O * b + o)), c)
    return {"y": y}

@@ -1,0 +1,406 @@
+from concourse.bass import DstId, RemoteDMATransfer
+from concourse.mybir import dt, AluOpType as A, AxisListType, ActivationFunctionType as F
+
+N, C, P, DS = 8, 128, 256, 80
+OFF = 16
+WIN = OFF + 5 * DS
+SH = 2048
+DUMP = 4112
+TAB = DUMP + 4096 + 5 * C + 16
+BIG = 1.0e6
+
+f32, bf, i32, u16, u8, c4 = "float32", "bfloat16", "int32", "uint16", "uint8", "float8_e4m3fn_x4"
+SCRATCH = {}
+for _n, _w, _d in [
+    ("one", 32, f32), ("onei", 8, i32),
+    ("ct", 8, i32), ("tabf", 8, f32), ("tot", 32, f32), ("it8", 8, f32), ("offc", 8, u16),
+    ("fm", 144, f32), ("dg", 256, f32), ("fm8", 40, f32), ("rst8", 40, f32),
+    ("i16", 8, f32), ("k8", 8, f32), ("ikh", 8, f32), ("ik2", 8, f32), ("idump", 40, f32), ("di", 40, f32),
+    ("pw", 8, f32), ("c5", 8, f32), ("c5h", 8, f32), ("kt5", 8, f32), ("thr", 8, f32),
+    ("bc", 128, bf), ("nrow", 128, bf), ("erow", 136, f32), ("nz", 128, bf), ("zrow", 128, bf),
+    ("se", 128, f32), ("et", 12, f32), ("fl8", 8, f32), ("de", 8, f32), ("vv", 8, f32), ("pkf", 8, f32), ("pk", 4, u16),
+    ("junk", 1024, f32), ("acc", 8, f32), ("comp", 8, u16), ("ce", 128, f32), ("nce", 2 * C, f32),
+    ("junl", 5 * C, f32), ("junp", 16, f32),
+    ("lsa", 12, u16), ("lfb", 12, f32), ("lsb", 12, u16), ("lfo", 6, f32), ("lso", 6, u16),
+    ("l2", 20, u16), ("wi", 20, i32), ("dei", 40, i32), ("fli", 40, i32), ("def_", 40, f32), ("fd", 40, f32),
+    ("prx", 40, f32), ("er", 40, f32), ("po", 40, f32), ("pos", 40, u16),
+    ("slots", 5 * C, bf), ("mr2", TAB, bf), ("mk", 256, bf), ("g", 256, f32), ("sgm", 256, f32), ("mn", 16, f32),
+    ("fin", 16, u16),
+    ("xb", 512, bf), ("xq", 128, c4), ("xs", 128, u8), ("xc", C + DS, c4), ("xcs", C + DS, u8),
+    ("spa", 2 * DS, c4), ("spas", 2 * DS, u8), ("spb", 2 * DS, c4), ("spbs", 2 * DS, u8),
+    ("win", WIN, c4), ("wins", WIN, u8), ("t2", 256, c4), ("t2s", 256, u8),
+    ("wb", 2048, bf), ("wq", 512, c4), ("ws", 512, u8), ("ysb", 512, f32),
+    ("r1b", 1, f32), ("r2b", 4, u16), ("rcb", DS, c4), ("rsb", DS, u8),
+]:
+    SCRATCH[_n] = ("sbuf", [128, _w], _d)
+ONE = {k: i for i, k in enumerate(["paf", "paf5", "paf2", "pgf", "sg", "pa", "ia", "a0", "a1", "a2", "a3", "a4"])}
+ONEI = {k: i for i, k in enumerate(["ip", "ipa", "ipg"])}
+SCRATCH["ps"] = ("psum", [128, 2048], f32)
+SEMAPHORES = (["cl", "xl", "wl", "l2d", "pad", "vs", "ss", "ts", "gs", "ls", "m2", "dc", "dsc",
+               "r1", "r2", "rc", "rsc", "st0"] + ["m1_%d" % s for s in range(N)])
+
+
+def needs(q):
+    return list(range(q)) if q < N // 2 else list(range(q + 1, N))
+
+
+def first(q):
+    return max(0, q - 2)
+
+
+def base(s, q):
+    return OFF + DS * (s - first(q))
+
+
+def plan(T, topo):
+    out = []
+    for r in range(N):
+        core = T.cores[r]
+        near = [q for q in (r - 1, r + 1, r - 2, r + 2) if 0 <= q < N]
+        far = [q for q in range(N) if q not in near and q != r and r in needs(q)]
+        direct = [q for q in near if topo.may_write(core, T.cores[q])]
+        hop = [q for q in near if q not in direct]
+        relays = [c for c in topo.cores_of(core) if c != core and all(topo.may_write(c, T.cores[q]) for q in hop + far)]
+        X = [c for c in relays if topo.die(c) == topo.die(core)][0]
+        Y = [c for c in relays if topo.die(c) != topo.die(core)][0]
+        out.append({"direct": direct, "hop": hop, "hop1": hop + far, "X": X, "Y": Y})
+    return out
+
+
+def mask_of(es):
+    return sum(1 << e for e in es)
+
+
+def part(es, k, n):
+    w = len(es) // n
+    return es[k * w:k * w + w]
+
+
+def sender(g, core, T, topo):
+    def send(items, rsem):
+        tr = []
+        for dst, es, o, i in items:
+            rid, pid = topo.addr(dst, core)
+            tr.append(RemoteDMATransfer(dst_ids=[DstId(rid=rid, pnc=pid)], dma_engine_mask=mask_of(es),
+                                        remote_sem=T.sem[rsem], src=i, dst=o))
+        g.remote_dma_fused(tr, local_sem=T.sem["ls"])
+        return sum(len(es) for _, es, _, _ in items)
+    return send
+
+
+def codes(v):
+    return v.bitcast(dt.uint8)
+
+
+def relay_program(g, core, T, topo, pl, r, isx):
+    me = pl[r]
+    send = sender(g, core, T, topo)
+    n = 0
+    dsts = me["hop1"] if isx else me["hop"]
+    g.wait_ge(T.sem["r1" if isx else "r2"], 8)
+    it = []
+    for k, q in enumerate(dsts):
+        dst = T.cores[q]
+        es = part(topo.engines(core, dst), k, len(dsts))
+        if isx:
+            it.append((dst, es, T.tot[:, 4 * r:4 * r + 1], T.r1b[:]))
+        else:
+            o = 4 * (r - first(q))
+            it.append((dst, es, T.l2[:, o:o + 4], T.r2b[:]))
+    n += send(it, "m1_%d" % r if isx else "m2")
+    for k, q in enumerate(me["hop"]):
+        if (k == 0) == isx:
+            dst = T.cores[q]
+            es = topo.engines(core, dst)
+            b = base(r, q)
+            g.wait_ge(T.sem["rc"], 8)
+            n += send([(dst, es, codes(T.win[:, b:b + DS]), codes(T.rcb[:]))], "dc")
+            g.wait_ge(T.sem["rsc"], 8)
+            n += send([(dst, es, T.wins[:, b:b + DS], T.rsb[:])], "dsc")
+    g.wait_ge(T.sem["ls"], n)
+
+
+def rank_program(g, core, T, topo):
+    pl = plan(T, topo)
+    r = T.rank_of(core)
+    if r is None:
+        for k in range(N):
+            if core == pl[k]["X"]:
+                relay_program(g, core, T, topo, pl, k, True)
+            if core == pl[k]["Y"]:
+                relay_program(g, core, T, topo, pl, k, False)
+        return
+    me = pl[r]
+    send = sender(g, core, T, topo)
+    queues = {"v": g.vector, "s": g.scalar, "t": g.tensor, "g": g, "y": g.sync}
+    own = {"v": "vs", "s": "ss", "t": "ts", "g": "gs"}
+    count = {"v": 0, "s": 0, "t": 0, "g": 0}
+    ev, seen, final = {}, {}, {}
+
+    def need(q, *keys):
+        m = {}
+        for k in keys:
+            s, v = ev[k]
+            m[s] = max(m.get(s, 0), v)
+        for s, v in m.items():
+            if seen.get((q, s), 0) < v:
+                queues[q].wait_ge(T.sem[s], v)
+                seen[(q, s)] = v
+
+    def do(q, fn, reads, write, *a, **kw):
+        need(q, *reads)
+        fn(*a, **kw).then_inc(T.sem[own[q]], 1)
+        count[q] += 1
+        ev[write] = (own[q], count[q])
+
+    def dma(q, reads, write, sem, out, in_):
+        need(q, *reads)
+        queues[q].dma_start(out, in_).then_inc(T.sem[sem], 16)
+        final[sem] = final.get(sem, 0) + 16
+        ev[write] = (sem, final[sem])
+
+    V, S = g.vector, g.scalar
+    X = AxisListType.X
+    one = {k: T.one[:, i:i + 1] for k, i in ONE.items()}
+    onei = {k: T.onei[:, i:i + 1] for k, i in ONEI.items()}
+    paf = one["paf"]
+    up = r >= N // 2
+    fi, hi = first(r), min(N - 1, r + 2)
+    n = hi - fi + 1
+    m = 8 * n
+
+    def iota(name, pattern, base_=0, out=None, reads=()):
+        do("g", g.iota, reads, name, T[name][:] if out is None else out, pattern, base_, 0,
+           allow_small_or_imprecise_dtypes=True)
+
+    def act(reads, write, out, in_, func=F.Identity, **kw):
+        do("s", S.activation, reads, write, out, in_, func, **kw)
+
+    for k in range(4):
+        for q, j in (("y", 2 * k), ("s", 2 * k + 1)):
+            dma(q, (), "ct", "cl", T.ct[16 * j:16 * j + 16, 0:8], T.cnt[:])
+    dma("y", (), "xb", "xl", T.xb[:], T.x[:])
+    dma("y", (), "wb", "wl", T.wb[:], T.w[:])
+
+    do("g", g.iota, (), "ip", onei["ip"], [[1, 1]], 0, 1)
+    iota("it8", [[2, 4], [0, 2]])
+    iota("fm", [[0, 9], [1, 16]])
+    iota("er0", [[0, 1]], 0, T.erow[:, 7:8])
+    iota("et0", [[0, 1]], 0, T.et[:, 0:1])
+    iota("i16", [[16, 8]])
+    iota("pw", [[0, 4], [256, 2]])
+    iota("c5", [[P, 5]], (r - 2) * P - (N * P if up else 0), T.c5[:, 0:5])
+    do("v", V.tensor_scalar, ("ip",), "ipa", onei["ipa"], onei["ip"], 15, None, A.bitwise_and)
+    do("v", V.tensor_scalar, ("ip",), "ipg", onei["ipg"], onei["ip"], 4, 1, A.logical_shift_right, A.bitwise_and)
+    do("v", V.tensor_copy, ("ipa",), "paf", paf, onei["ipa"])
+    do("v", V.tensor_copy, ("ipg",), "pgf", one["pgf"], onei["ipg"])
+    do("v", V.tensor_scalar, ("it8", "pgf"), "offc", T.offc[:], T.it8[:], one["pgf"], None, A.add)
+    do("v", V.tensor_scalar, ("fm", "paf"), "dg", T.dg[:, 0:128], T.fm[:, 1:129], paf, BIG, A.is_equal, A.mult)
+    act(("paf",), "paf5", one["paf5"], paf, bias=0.5)
+    act(("i16", "paf5"), "k8", T.k8[:], T.i16[:], bias=one["paf5"])
+    act(("c5",), "c5h", T.c5h[:, 0:5], T.c5[:, 0:5], bias=0.5)
+
+    end = T.erow[:, 8:136]
+    mine = T.erow[:, 135:136]
+    do("v", V.tensor_copy, ("ct", "offc"), "bc", T.bc[:], T.ct[:, 0:8].indirect(T.offc[:]))
+    do("v", V.tensor_copy, ("ct",), "tabf", T.tabf[:], T.ct[:])
+    do("v", V.transpose, ("bc",), "nrow", T.nrow[:], T.bc[:])
+    act(("tabf",), "fl8", T.fl8[:], T.tabf[:], F.Relu, scale=-128.0, bias=128.0)
+    act(("nrow",), "nz", T.nz[:], T.nrow[:], F.Sign)
+    do("v", V.tensor_tensor_scan, ("nrow",), "erow", end, T.nrow[:], T.nrow[:], 0.0, A.add, A.max)
+
+    nls = 0
+    need("g", "erow")
+    chip, chipy = part(topo.engines(core, me["X"]), 0, 2), part(topo.engines(core, me["Y"]), 1, 2)
+    dr, hop = me["direct"], me["hop"]
+
+    def direct_engines(k):
+        return part(topo.engines(core, T.cores[dr[k]]), k, len(dr))
+    nls += send([(me["X"], chip, T.r1b[:], mine)], "r1")
+    nls += send([(T.cores[q], direct_engines(k), T.tot[:, 4 * r:4 * r + 1], mine) for k, q in enumerate(dr)], "m1_%d" % r)
+
+    do("v", V.tensor_tensor_scan, ("erow", "er0", "dg"), "se", T.se[:], T.erow[:, 7:135], T.dg[:, 0:128], BIG, A.min, A.max)
+    do("v", V.tensor_tensor_scan, ("nz",), "zrow", T.zrow[:], T.nz[:], T.nz[:], 0.0, A.add, A.max)
+    act(("erow",), "tot", T.tot[:, 4 * r:4 * r + 1], mine, F.Copy)
+    kt, ktk = T.c5h, "c5h"
+    if up:
+        act(("c5h", "erow"), "kt5", T.kt5[:, 0:5], T.c5h[:, 0:5], bias=mine)
+        kt, ktk = T.kt5, "kt5"
+    for c in range(8):
+        act(("zrow", "k8"), "acc", T.junk[:, 128 * c:128 * c + 127], T.zrow[:, 0:127], F.Sign,
+            bias=T.k8[:, c:c + 1], scale=-1.0, accum_out=T.acc[:, c:c + 1])
+    do("v", V.tensor_tensor, ("se",), "et", T.et[:, 1:9], T.se[:, 14:128:16], T.se[:, 15:128:16], A.min)
+    do("v", V.tensor_tensor, ("et", "et0"), "de", T.de[:], T.et[:, 1:9], T.et[:, 0:8], A.subtract)
+    do("v", V.tensor_tensor, ("de", "fl8"), "vv", T.vv[:], T.de[:], T.fl8[:], A.add)
+    do("v", V.tensor_tensor_scan, ("vv", "pw"), "pkf", T.pkf[:], T.pw[:], T.vv[:], 0.0, A.mult, A.add)
+    do("v", V.tensor_copy, ("pkf",), "pk", T.pk[:], T.pkf[:, 1:8:2])
+
+    need("g", "pk")
+    nls += send([(me["Y"], chipy, T.r2b[:], T.pk[:])], "r2")
+    nls += send([(T.cores[q], direct_engines(k), T.l2[:, 4 * (r - first(q)):4 * (r - first(q)) + 4], T.pk[:])
+                 for k, q in enumerate(dr)], "m2")
+    o = 4 * (r - fi)
+    dma("y", ("pk",), "l2own", "l2d", T.l2[:, o:o + 4], T.pk[:])
+
+    do("v", V.quantize_mx, ("xb",), "xq", T.xq[:], T.xs[:], T.xb[:])
+    do("v", V.memset, (), "mr0", T.mr2[:, SH:SH + P], 0.0)
+    do("v", V.tensor_scalar, ("fm", "paf"), "dg2", T.dg[:, 128:256], T.fm[:, 1:129], paf, BIG, A.is_equal, A.mult)
+    do("v", V.tensor_scalar, ("acc",), "comp", T.comp[:], T.acc[:], 0.5, 63.5, A.mult, A.add)
+    for k in range(2):
+        do("v", V.memset, (), "slots", T.slots[:, C * k:C * k + C], float(OFF + DS * k))
+    do("v", V.tensor_copy, ("xq", "comp"), "xc", T.xc[:, 0:C].bitcast(dt.uint32), T.xq[:].bitcast(dt.uint32).indirect(T.comp[:, 0:8]))
+    act(("erow", "comp"), "ce", T.ce[:], end.indirect(T.comp[:, 0:8]), F.Copy)
+    act(("xq", "comp"), "xcs", T.xcs[:, 0:C], T.xs[:].indirect(T.comp[:, 0:8]), F.Copy)
+    for k in range(2, n):
+        do("v", V.memset, (), "slots", T.slots[:, C * k:C * k + C], float(OFF + DS * k))
+    do("v", V.quantize_mx, ("wb",), "wq", T.wq[:], T.ws[:], T.wb[:])
+    dma("y", ("xq",), "xpad", "pad", codes(T.xc[:, C:C + DS]), codes(T.xq[:, 0:DS]))
+    dma("y", ("xq",), "xpad", "pad", T.xcs[:, C:C + DS], T.xs[:, 0:DS])
+
+    iota("ikh", [[16, 8]])
+    iota("prz", [[0, 40]], 0, T.prx[:])
+    if r < 3:
+        iota("pr0", [[0, 1]], SH - r * P, T.prx[:, 0:1], reads=("prz",))
+    iota("fm8", [[0, 5], [1, 8]])
+    iota("idump", [[16, 40]], DUMP)
+    act(("paf",), "paf2", one["paf2"], paf, scale=2.0, bias=127.0)
+    act(("ikh", "paf2"), "ik2", T.ik2[:], T.ikh[:], scale=2.0, bias=one["paf2"])
+    for i, q in enumerate(hop):
+        d = q - (r - 2)
+        act(("ce", ktk), "nce", T.nce[:, C * i:C * i + 127], T.ce[:, 0:127], scale=-1.0, bias=kt[:, d:d + 1])
+    act(("fm8",), "rst8", T.rst8[:], T.fm8[:], F.Sign)
+    act(("idump", "paf"), "di", T.di[:], T.idump[:], bias=paf)
+
+    n2, nd = 0, 0
+    for s in range(N):
+        for kind in ("hop1", "direct"):
+            if r in pl[s][kind]:
+                ev["m1_%d" % s] = ("m1_%d" % s, 8 // len(pl[s][kind]))
+        if r in pl[s]["hop"]:
+            n2 += 8 // len(pl[s]["hop"])
+            nd += 8
+        elif r in pl[s]["direct"]:
+            n2 += 8 // len(pl[s]["direct"])
+            nd += 8 // len(pl[s]["direct"])
+    ev["m2"], ev["dc"], ev["dsc"] = ("m2", n2), ("dc", nd), ("dsc", nd)
+
+    ns = needs(r)
+    if ns:
+        act(["m1_%d" % s for s in ns], "sg", T.junp[:, 8:8 + len(ns)], T.tot[:, 4 * ns[0]:4 * ns[-1] + 1:4], F.Copy,
+            scale=1.0 if up else -1.0, accum_out=one["sg"])
+
+    if r == 3:
+        do("v", V.tensor_scalar, ("prz", "m1_0"), "pr0", T.prx[:, 0:1], T.tot[:, 0:1], float(SH - r * P), None, A.add)
+    elif up:
+        do("v", V.tensor_reduce, ["m1_%d" % s for s in range(fi, N) if s != r] + ["tot"], "pa", one["pa"],
+           T.tot[:, 4 * fi:4 * (N - 1) + 1:4], X, A.add)
+        do("v", V.tensor_scalar, ("prz", "pa"), "pr0", T.prx[:, 0:1], one["pa"], -1.0, float(SH + (N - r) * P), A.mult, A.add)
+    steps = T.tot[:, 4 * fi:4 * (hi - 1) + 1:4]
+    do("v", V.tensor_tensor_scan, ["m1_%d" % s for s in range(fi, hi) if s != r] + ["tot", "pr0", "prz"], "prx",
+       T.prx[:, 8:8 * (n - 1) + 1:8], steps, steps, T.prx[:, 0:1], A.add, A.max)
+
+    for i, q in enumerate(hop):
+        d = q - (r - 2)
+        row = T.nce[:, C * i:C * i + 127]
+        if ns:
+            act(("nce", "sg"), "a%d" % d, T.junl[:, C * d:C * d + 127], row, F.Sign, bias=one["sg"], accum_out=one["a%d" % d])
+        else:
+            act(("nce",), "a%d" % d, T.junl[:, C * d:C * d + 127], row, F.Sign, accum_out=one["a%d" % d])
+    thr, tk = kt, ktk
+    if ns:
+        act((ktk, "sg"), "thr", T.thr[:, 0:5], kt[:, 0:5], bias=one["sg"])
+        thr, tk = T.thr, "thr"
+
+    def counts(dsts):
+        for q in dsts:
+            d = q - (r - 2)
+            act(("ce", tk), "a%d" % d, T.junl[:, C * d:C * d + 127], T.ce[:, 0:127], F.Sign,
+                bias=thr[:, d:d + 1], scale=-1.0, accum_out=one["a%d" % d])
+
+    def lists(dsts, lf, name):
+        for i, q in enumerate(dsts):
+            d = q - (r - 2)
+            act(("ik2", "a%d" % d), name + "f", lf[:, 5 * i:5 * i + 5], T.ik2[:, 0:5], bias=one["a%d" % d])
+
+    def clamp(k, lf, ls, name):
+        do("v", V.tensor_scalar, (name + "f",), name, ls[:, 0:5 * k], lf[:, 0:5 * k], 0.5, 127.0, A.mult, A.min)
+
+    def pick(k, dst, ls, name, *keys):
+        do("v", V.tensor_copy, ("xc", name) + keys, name + "c", dst.bitcast(dt.uint32),
+           T.xc[:, 0:C + DS * len(keys)].bitcast(dt.uint32).indirect(ls[:, 0:5 * k]))
+
+    def picks(k, dst, ls, name, *keys):
+        act(("xcs", name) + keys, name + "s", dst, T.xcs[:, 0:C + DS * len(keys)].indirect(ls[:, 0:5 * k]), F.Copy)
+    ka, kb = len(hop), len(dr)
+    counts(dr[:1])
+    for i, q in enumerate(hop):
+        a = "a%d" % (q - (r - 2))
+        do("v", V.tensor_scalar, ("ik2", a), "la", T.lsa[:, 5 * i:5 * i + 5], T.ik2[:, 0:5], one[a], 0.5, A.add, A.mult)
+    pick(ka, T.spa[:, 0:DS * ka], T.lsa, "la", "xpad")
+    picks(ka, T.spas[:, 0:DS * ka], T.lsa, "la", "xpad")
+    relay = [(me["X"], chip), (me["Y"], chipy)]
+    need("g", "lac")
+    nls += send([(c, es, codes(T.rcb[:]), codes(T.spa[:, DS * i:DS * i + DS])) for i, (c, es) in enumerate(relay[:ka])], "rc")
+    need("g", "las")
+    nls += send([(c, es, T.rsb[:], T.spas[:, DS * i:DS * i + DS]) for i, (c, es) in enumerate(relay[:ka])], "rsc")
+    counts(dr[1:])
+    lists(dr, T.lfb, "lb")
+    counts([r])
+    lists([r], T.lfo, "lo")
+    act(("prx",), "ia", T.junp[:, 0:n - 1], T.prx[:, 8:8 * (n - 1) + 1:8], F.Sign, scale=-1.0, bias=SH + 0.5, accum_out=one["ia"])
+
+    do("v", V.tensor_copy, ("m2", "l2own"), "wi", T.wi[:, 0:4 * n], T.l2[:, 0:4 * n])
+    wi = T.wi[:, 0:4 * n]
+    do("v", V.tensor_scalar, ("wi",), "dei", T.dei[:, 1:m:2], wi, 127, None, A.bitwise_and)
+    do("v", V.tensor_scalar, ("wi",), "dei2", T.dei[:, 0:m:2], wi, 8, 127, A.logical_shift_right, A.bitwise_and)
+    do("v", V.tensor_scalar, ("wi",), "fli", T.fli[:, 1:m:2], wi, 7, 1, A.logical_shift_right, A.bitwise_and)
+    do("v", V.tensor_scalar, ("wi",), "fli2", T.fli[:, 0:m:2], wi, 15, None, A.logical_shift_right)
+    do("v", V.tensor_tensor, ("dei2", "prx"), "def_", T.def_[:, 0:m], T.dei[:, 0:m], T.prx[:, 0:m], A.add)
+    do("v", V.tensor_tensor, ("fli2", "di"), "fd", T.fd[:, 0:m], T.fli[:, 0:m], T.di[:, 0:m], A.mult)
+    clamp(kb, T.lfb, T.lsb, "lb")
+    do("v", V.tensor_tensor_scan, ("def_", "rst8"), "er", T.er[:, 0:m], T.rst8[:, 0:m], T.def_[:, 0:m], 0.0, A.mult, A.add)
+    pick(kb, T.spb[:, 0:DS * kb], T.lsb, "lb")
+    picks(kb, T.spbs[:, 0:DS * kb], T.lsb, "lb")
+    need("g", "lbc")
+    nls += send([(T.cores[q], direct_engines(i), codes(T.win[:, base(r, q):base(r, q) + DS]), codes(T.spb[:, DS * i:DS * i + DS]))
+                 for i, q in enumerate(dr)], "dc")
+    need("g", "lbs")
+    nls += send([(T.cores[q], direct_engines(i), T.wins[:, base(r, q):base(r, q) + DS], T.spbs[:, DS * i:DS * i + DS])
+                 for i, q in enumerate(dr)], "dsc")
+    do("v", V.tensor_tensor, ("er", "fd"), "po", T.po[:, 0:m], T.er[:, 0:m], T.fd[:, 0:m], A.add)
+    clamp(1, T.lfo, T.lso, "lo")
+    do("v", V.tensor_copy, ("po",), "pos", T.pos[:, 0:m], T.po[:, 0:m])
+    act(("ia",), "g0", T.g[:, 0:1], one["ia"], scale=DS / 2.0, bias=float(OFF + DS * (n - 1) // 2))
+
+    do("v", V.tensor_copy, ("pos", "slots", "mr0"), "mr2", T.mr2[:].indirect(T.pos[:, 0:m]), T.slots[:, 0:16 * m])
+    b = base(r, r)
+    pick(1, T.win[:, b:b + DS], T.lso, "lo")
+    picks(1, T.wins[:, b:b + DS], T.lso, "lo")
+    do("v", V.tensor_scalar, ("mr2",), "mk", T.mk[:], T.mr2[:, SH:SH + P], 0.0, None, A.is_gt)
+    do("v", V.tensor_tensor_scan, ("mk", "g0"), "g", T.g[:, 1:P], T.mk[:, 1:P], T.mr2[:, SH + 1:SH + P], T.g[:, 0:1], A.add, A.max)
+    do("v", V.tensor_tensor_scan, ("g", "dg2"), "sgm", T.sgm[:], T.g[:], T.dg[:], BIG, A.min, A.max)
+    do("v", V.tensor_tensor, ("sgm",), "mn", T.mn[:], T.sgm[:, 14:256:16], T.sgm[:, 15:256:16], A.min)
+    do("v", V.tensor_copy, ("mn",), "fin", T.fin[:], T.mn[:])
+
+    for b in (0, 1):
+        do("v", V.tensor_copy, ("dc", "loc", "fin"), "t%d" % b, T.t2[:, 128 * b:128 * b + 128].bitcast(dt.uint32),
+           T.win[:].bitcast(dt.uint32).indirect(T.fin[:, 8 * b:8 * b + 8]))
+        act(("dsc", "los", "fin"), "t%ds" % b, T.t2s[:, 128 * b:128 * b + 128],
+            T.wins[:].indirect(T.fin[:, 8 * b:8 * b + 8]), F.Copy)
+    for b in (0, 1):
+        for o in (0, 1):
+            k = 2 * b + o
+            do("t", g.tensor.matmul_mx, ("wq", "t%d" % b, "t%ds" % b), "mm%d" % k, T.ps[:, 512 * k:512 * k + 128],
+               T.wq[:, 128 * k:128 * k + 128], T.ws[:, 128 * k:128 * k + 128],
+               T.t2[:, 128 * b:128 * b + 128], T.t2s[:, 128 * b:128 * b + 128], True, True)
+    for b in (0, 1):
+        do("v", V.tensor_copy, ("mm%d" % (2 * b),), "y0", T.ysb[:, 128 * b:128 * b + 128], T.ps[:, 1024 * b:1024 * b + 128])
+        act(("mm%d" % (2 * b + 1),), "y1", T.ysb[:, P + 128 * b:P + 128 * b + 128], T.ps[:, 1024 * b + 512:1024 * b + 640], F.Copy)
+    dma("y", ("y0", "y1"), "st0", "st0", T.y[:], T.ysb[:])
+
+    for q, s in own.items():
+        ev["end_" + q] = (s, count[q])
+    for s, v in final.items():
+        ev["end_" + s] = (s, v)
+    ev["end_ls"] = ("ls", nls)
+    need("g", *[k for k in ev if k.startswith("end_") or k.startswith("m1_")], "m2", "dc", "dsc")

@@ -1,69 +1,92 @@
 from concourse.bass import DstId, RemoteDMATransfer
-from concourse.mybir import dt, AluOpType as A, AxisListType, ActivationFunctionType as F
+from concourse.mybir import dt, AluOpType as A, ActivationFunctionType as F
 
 N, C, P, DS = 8, 128, 256, 80
-OFF = 16
-WIN = OFF + 5 * DS
-SH = 2048
-DUMP = 4112
-TAB = DUMP + 4096 + 5 * C + 16
+REST = C - DS
+WIN = 4 * DS + 2 * C
+BACK = 5
+SH = 4 * P + 16
+DUMP = SH + 5 * P + 16
+TAB = 2 * DUMP + N * C
 BIG = 1.0e6
 
 f32, bf, i32, u16, u8, c4 = "float32", "bfloat16", "int32", "uint16", "uint8", "float8_e4m3fn_x4"
 SCRATCH = {}
 for _n, _w, _d in [
     ("one", 32, f32), ("onei", 8, i32),
-    ("ct", 8, i32), ("tabf", 8, f32), ("tot", 32, f32), ("it8", 8, f32), ("offc", 8, u16),
-    ("fm", 144, f32), ("dg", 256, f32), ("fm8", 40, f32), ("rst8", 40, f32),
-    ("i16", 8, f32), ("k8", 8, f32), ("ikh", 8, f32), ("ik2", 8, f32), ("idump", 40, f32), ("di", 40, f32),
-    ("pw", 8, f32), ("c5", 8, f32), ("c5h", 8, f32), ("kt5", 8, f32), ("thr", 8, f32),
-    ("bc", 128, bf), ("nrow", 128, bf), ("erow", 136, f32), ("nz", 128, bf), ("zrow", 128, bf),
-    ("se", 128, f32), ("et", 12, f32), ("fl8", 8, f32), ("de", 8, f32), ("vv", 8, f32), ("pkf", 8, f32), ("pk", 4, u16),
-    ("junk", 1024, f32), ("acc", 8, f32), ("comp", 8, u16), ("ce", 128, f32), ("nce", 2 * C, f32),
-    ("junl", 5 * C, f32), ("junp", 16, f32),
-    ("lsa", 12, u16), ("lfb", 12, f32), ("lsb", 12, u16), ("lfo", 6, f32), ("lso", 6, u16),
-    ("l2", 20, u16), ("wi", 20, i32), ("dei", 40, i32), ("fli", 40, i32), ("def_", 40, f32), ("fd", 40, f32),
-    ("prx", 40, f32), ("er", 40, f32), ("po", 40, f32), ("pos", 40, u16),
-    ("slots", 5 * C, bf), ("mr2", TAB, bf), ("mk", 256, bf), ("g", 256, f32), ("sgm", 256, f32), ("mn", 16, f32),
-    ("fin", 16, u16),
-    ("xb", 512, bf), ("xq", 128, c4), ("xs", 128, u8), ("xc", C + DS, c4), ("xcs", C + DS, u8),
-    ("spa", 2 * DS, c4), ("spas", 2 * DS, u8), ("spb", 2 * DS, c4), ("spbs", 2 * DS, u8),
-    ("win", WIN, c4), ("wins", WIN, u8), ("t2", 256, c4), ("t2s", 256, u8),
+    ("ct", 8, i32), ("cu", 8, u16), ("t8", 8, f32), ("i16", 8, f32), ("k8", 8, f32), ("k8k", 8, f32), ("k8b", 8, bf), ("j16", 8, f32),
+    ("j80", 8, f32), ("i32", 4, f32), ("t32", 4, f32), ("di", 4, f32), ("fl", 4, f32), ("dmp", 4, f32), ("pf", 4, f32),
+    ("i64", 64, f32), ("t64", 64, f32), ("fm", P, bf), ("dg", P, bf),
+    ("nrow", C, bf), ("nz", C, bf), ("erow", C + 8, f32), ("zrow", C, bf),
+    ("junk", 4 * C, f32), ("acc", 4, f32), ("rm", 4 * C, bf), ("cmp", 4 * C, bf), ("cs", 4 * C, bf), ("comp", 8, u16),
+    ("ce", C, f32), ("cet", C, f32), ("msg", 8 * N, u16), ("tf", 8, f32), ("zer", 8, f32), ("sc", 8, f32),
+    ("l80", 6, u16), ("pos", 20, u16), ("val", 5 * 64, f32), ("tab", TAB, f32), ("run", P + 8, f32), ("held", 2 * P, f32),
+    ("ya", 32, f32), ("yb", 32, f32), ("yc", 32, f32), ("fin", 16, u16),
+    ("xb", 512, bf), ("xq", C, c4), ("xs", C, u8), ("xc", C, c4), ("xcs", C, u8),
+    ("sp", DS, c4), ("sps", DS, u8), ("late", DS, c4), ("lates", DS, u8),
+    ("wine", WIN, c4), ("wines", WIN, u8), ("winm", WIN, c4), ("winms", WIN, u8), ("t2", P, c4), ("t2s", P, u8),
     ("wb", 2048, bf), ("wq", 512, c4), ("ws", 512, u8), ("ysb", 512, f32),
-    ("r1b", 1, f32), ("r2b", 4, u16), ("rcb", DS, c4), ("rsb", DS, u8),
+    ("r1b", 2, u16), ("r2b", 4, u16), ("rcb", C, c4), ("rsb", C, u8),
 ]:
     SCRATCH[_n] = ("sbuf", [128, _w], _d)
-ONE = {k: i for i, k in enumerate(["paf", "paf5", "paf2", "pgf", "sg", "pa", "ia", "a0", "a1", "a2", "a3", "a4"])}
-ONEI = {k: i for i, k in enumerate(["ip", "ipa", "ipg"])}
+ONE = {k: i for i, k in enumerate(["paf", "puf", "h16", "paf5", "mm", "dl", "dv", "sg", "ba", "bb", "b0", "b1", "b2", "b3", "b4"])}
+ONEI = {k: i for i, k in enumerate(["ip", "ipa", "ipu"])}
 SCRATCH["ps"] = ("psum", [128, 2048], f32)
-SEMAPHORES = (["cl", "xl", "wl", "l2d", "pad", "vs", "ss", "ts", "gs", "ls", "m2", "dc", "dsc",
-               "r1", "r2", "rc", "rsc", "st0"] + ["m1_%d" % s for s in range(N)])
+SEMAPHORES = ["cl", "xl", "wl", "own", "dup", "vs", "ss", "ts", "gs", "ls", "m1", "m2", "md", "cd", "sd",
+              "c1", "s1", "c2", "s2", "r1", "r2", "rc", "rsc", "st"]
+
+
+def up(r):
+    return r >= N // 2
+
+
+def mid(q):
+    return 2 <= q < N - 2
+
+
+def sources(q):
+    return list(range(max(0, q - 2), min(N, q + 3)))
 
 
 def needs(q):
-    return list(range(q)) if q < N // 2 else list(range(q + 1, N))
+    return range(sources(q)[0], N) if up(q) else range(sources(q)[-1])
 
 
-def first(q):
-    return max(0, q - 2)
+def short(q):
+    return (q + 1, q + 2) if up(q) else (q - 1, q - 2)
 
 
-def base(s, q):
-    return OFF + DS * (s - first(q))
+def layout(q):
+    out, at = {}, 0
+    if mid(q) and not up(q):
+        out["dup"], at = 0, DS
+    if not mid(q) and up(q):
+        at = -DS % 32
+    for s in sources(q):
+        out[s] = at
+        at += DS if abs(s - q) == 2 or (mid(q) and s == short(q)[0]) else C
+    if mid(q) and up(q):
+        out["dup"] = at
+    return out
+
+
+def block(s, q):
+    return 8 * (N - 1 - s if up(q) else s)
 
 
 def plan(T, topo):
     out = []
     for r in range(N):
         core = T.cores[r]
-        near = [q for q in (r - 1, r + 1, r - 2, r + 2) if 0 <= q < N]
-        far = [q for q in range(N) if q not in near and q != r and r in needs(q)]
+        near = [q for q in sources(r) if q != r]
+        far = [q for q in range(N) if abs(q - r) > 2 and r in needs(q)]
         direct = [q for q in near if topo.may_write(core, T.cores[q])]
         hop = [q for q in near if q not in direct]
         relays = [c for c in topo.cores_of(core) if c != core and all(topo.may_write(c, T.cores[q]) for q in hop + far)]
         X = [c for c in relays if topo.die(c) == topo.die(core)][0]
         Y = [c for c in relays if topo.die(c) != topo.die(core)][0]
-        out.append({"direct": direct, "hop": hop, "hop1": hop + far, "X": X, "Y": Y})
+        dst = (hop[::-1] if up(r) else hop) + far
+        out.append({"direct": direct, "hop": hop, "relay": list(zip((X, Y), dst))})
     return out
 
 
@@ -77,14 +100,14 @@ def part(es, k, n):
 
 
 def sender(g, core, T, topo):
-    def send(items, rsem):
+    def send(items):
         tr = []
-        for dst, es, o, i in items:
+        for dst, es, o, i, rsem in items:
             rid, pid = topo.addr(dst, core)
             tr.append(RemoteDMATransfer(dst_ids=[DstId(rid=rid, pnc=pid)], dma_engine_mask=mask_of(es),
                                         remote_sem=T.sem[rsem], src=i, dst=o))
         g.remote_dma_fused(tr, local_sem=T.sem["ls"])
-        return sum(len(es) for _, es, _, _ in items)
+        return sum(len(es) for _, es, _, _, _ in items)
     return send
 
 
@@ -92,31 +115,35 @@ def codes(v):
     return v.bitcast(dt.uint8)
 
 
-def relay_program(g, core, T, topo, pl, r, isx):
-    me = pl[r]
+def words(v):
+    return v.bitcast(dt.uint32)
+
+
+def window(T, q):
+    return (T.winm, T.winms) if mid(q) else (T.wine, T.wines)
+
+
+def ends(r):
+    return slice(REST, C) if up(r) else slice(0, DS)
+
+
+def relay_program(g, core, T, topo, r, q, got):
     send = sender(g, core, T, topo)
-    n = 0
-    dsts = me["hop1"] if isx else me["hop"]
-    g.wait_ge(T.sem["r1" if isx else "r2"], 8)
-    it = []
-    for k, q in enumerate(dsts):
-        dst = T.cores[q]
-        es = part(topo.engines(core, dst), k, len(dsts))
-        if isx:
-            it.append((dst, es, T.tot[:, 4 * r:4 * r + 1], T.r1b[:]))
-        else:
-            o = 4 * (r - first(q))
-            it.append((dst, es, T.l2[:, o:o + 4], T.r2b[:]))
-    n += send(it, "m1_%d" % r if isx else "m2")
-    for k, q in enumerate(me["hop"]):
-        if (k == 0) == isx:
-            dst = T.cores[q]
-            es = topo.engines(core, dst)
-            b = base(r, q)
-            g.wait_ge(T.sem["rc"], 8)
-            n += send([(dst, es, codes(T.win[:, b:b + DS]), codes(T.rcb[:]))], "dc")
-            g.wait_ge(T.sem["rsc"], 8)
-            n += send([(dst, es, T.wins[:, b:b + DS], T.rsb[:])], "dsc")
+    dst = T.cores[q]
+    es = topo.engines(core, dst)
+    o = block(r, q)
+    g.wait_ge(T.sem["r1"], got)
+    n = send([(dst, es, T.msg[:, o:o + 1], T.r1b[:, 0:1], "m1")])
+    if abs(q - r) == 1:
+        win, wins = window(T, q)
+        cut = ends(r) if mid(q) and short(q)[0] == r else slice(0, C)
+        b, w, side = layout(q)[r], cut.stop - cut.start, "1" if r < q else "2"
+        g.wait_ge(T.sem["r2"], got)
+        n += send([(dst, es, T.msg[:, o + 2:o + 6], T.r2b[:], "m2")])
+        g.wait_ge(T.sem["rc"], got)
+        n += send([(dst, es, codes(win[:, b:b + w]), codes(T.rcb[:, cut]), "c" + side)])
+        g.wait_ge(T.sem["rsc"], got)
+        n += send([(dst, es, wins[:, b:b + w], T.rsb[:, cut], "s" + side)])
     g.wait_ge(T.sem["ls"], n)
 
 
@@ -125,10 +152,9 @@ def rank_program(g, core, T, topo):
     r = T.rank_of(core)
     if r is None:
         for k in range(N):
-            if core == pl[k]["X"]:
-                relay_program(g, core, T, topo, pl, k, True)
-            if core == pl[k]["Y"]:
-                relay_program(g, core, T, topo, pl, k, False)
+            for c, q in pl[k]["relay"]:
+                if core == c:
+                    relay_program(g, core, T, topo, k, q, len(topo.engines(T.cores[k], c)) // 2)
         return
     me = pl[r]
     send = sender(g, core, T, topo)
@@ -160,21 +186,34 @@ def rank_program(g, core, T, topo):
         ev[write] = (sem, final[sem])
 
     V, S = g.vector, g.scalar
-    X = AxisListType.X
     one = {k: T.one[:, i:i + 1] for k, i in ONE.items()}
     onei = {k: T.onei[:, i:i + 1] for k, i in ONEI.items()}
-    paf = one["paf"]
-    up = r >= N // 2
-    fi, hi = first(r), min(N - 1, r + 2)
-    n = hi - fi + 1
-    m = 8 * n
+    src, lay = sources(r), layout(r)
+    n = len(src)
+    win, wins = window(T, r)
+    mo = block(r, r)
 
-    def iota(name, pattern, base_=0, out=None, reads=()):
-        do("g", g.iota, reads, name, T[name][:] if out is None else out, pattern, base_, 0,
-           allow_small_or_imprecise_dtypes=True)
+    def iota(name, pattern, base_=0):
+        do("g", g.iota, (), name, T[name][:], pattern, base_, 0, allow_small_or_imprecise_dtypes=True)
 
     def act(reads, write, out, in_, func=F.Identity, **kw):
         do("s", S.activation, reads, write, out, in_, func, **kw)
+
+    def ts(reads, write, *a):
+        do("v", V.tensor_scalar, reads, write, *a)
+
+    def tt(reads, write, *a):
+        do("v", V.tensor_tensor, reads, write, *a)
+
+    def scan(reads, write, *a):
+        do("v", V.tensor_tensor_scan, reads, write, *a)
+
+    def fill(write, ap, c):
+        do("v", V.memset, (), write, ap, c)
+
+    def pick(reads, name, dst, dsts, from_, froms, off):
+        do("v", V.tensor_copy, reads[0], name + "c", words(dst), words(from_).indirect(off))
+        act(reads[1], name + "s", dsts, froms.indirect(off), F.Copy)
 
     for k in range(4):
         for q, j in (("y", 2 * k), ("s", 2 * k + 1)):
@@ -183,224 +222,246 @@ def rank_program(g, core, T, topo):
     dma("y", (), "wb", "wl", T.wb[:], T.w[:])
 
     do("g", g.iota, (), "ip", onei["ip"], [[1, 1]], 0, 1)
-    iota("it8", [[2, 4], [0, 2]])
-    iota("fm", [[0, 9], [1, 16]])
-    iota("er0", [[0, 1]], 0, T.erow[:, 7:8])
-    iota("et0", [[0, 1]], 0, T.et[:, 0:1])
+    iota("t8", [[1, 8]])
     iota("i16", [[16, 8]])
-    iota("pw", [[0, 4], [256, 2]])
-    iota("c5", [[P, 5]], (r - 2) * P - (N * P if up else 0), T.c5[:, 0:5])
-    do("v", V.tensor_scalar, ("ip",), "ipa", onei["ipa"], onei["ip"], 15, None, A.bitwise_and)
-    do("v", V.tensor_scalar, ("ip",), "ipg", onei["ipg"], onei["ip"], 4, 1, A.logical_shift_right, A.bitwise_and)
-    do("v", V.tensor_copy, ("ipa",), "paf", paf, onei["ipa"])
-    do("v", V.tensor_copy, ("ipg",), "pgf", one["pgf"], onei["ipg"])
-    do("v", V.tensor_scalar, ("it8", "pgf"), "offc", T.offc[:], T.it8[:], one["pgf"], None, A.add)
-    do("v", V.tensor_scalar, ("fm", "paf"), "dg", T.dg[:, 0:128], T.fm[:, 1:129], paf, BIG, A.is_equal, A.mult)
-    act(("paf",), "paf5", one["paf5"], paf, bias=0.5)
+    iota("i32", [[32, 4]])
+    iota("i64", [[32, 4], [1, 16]])
+    iota("fm", [[0, 16], [1, 16]])
+    fill("rm1", T.rm[:], 1.0)
+    ts(("ip",), "ipa", onei["ipa"], onei["ip"], 15, None, A.bitwise_and)
+    ts(("ip",), "ipu", onei["ipu"], onei["ip"], 31, None, A.bitwise_and)
+    fill("er0", T.erow[:, 0:1], 0.0)
+    do("v", V.tensor_copy, ("ipa",), "paf", one["paf"], onei["ipa"])
+    do("v", V.tensor_copy, ("ipu",), "puf", one["puf"], onei["ipu"])
+    do("v", V.memset, ("rm1",), "rm", T.rm[:, 0:4 * C:C], 0.0)
+    fill("cmp0", T.cmp[:, 0:4 * C:C], 0.0)
+    fill("tab0", T.tab[:, SH - BACK:SH + P], 0.0)
+    fill("zer", T.zer[:], 0.0)
+    fill("held0", T.held[:, P + 15:2 * P:16], 0.0)
+    act(("paf",), "paf5", one["paf5"], one["paf"], bias=0.5 - (C if up(r) else 0))
     act(("i16", "paf5"), "k8", T.k8[:], T.i16[:], bias=one["paf5"])
-    act(("c5",), "c5h", T.c5h[:, 0:5], T.c5[:, 0:5], bias=0.5)
+    act(("i32", "puf"), "t32", T.t32[:], T.i32[:], bias=one["puf"])
+    act(("i16", "paf"), "j16", T.j16[:], T.i16[:], bias=one["paf"])
+    act(("j16",), "k8b", T.k8b[:], T.j16[:], bias=-float(C if up(r) else 0))
+    act(("paf", "puf"), "h16", one["h16"], one["paf"], scale=-1.0, bias=one["puf"])
+    act(("t32",), "di", T.di[:], T.t32[:], bias=float(DUMP + C * r))
 
-    end = T.erow[:, 8:136]
-    mine = T.erow[:, 135:136]
-    do("v", V.tensor_copy, ("ct", "offc"), "bc", T.bc[:], T.ct[:, 0:8].indirect(T.offc[:]))
-    do("v", V.tensor_copy, ("ct",), "tabf", T.tabf[:], T.ct[:])
-    do("v", V.transpose, ("bc",), "nrow", T.nrow[:], T.bc[:])
-    act(("tabf",), "fl8", T.fl8[:], T.tabf[:], F.Relu, scale=-128.0, bias=128.0)
-    act(("nrow",), "nz", T.nz[:], T.nrow[:], F.Sign)
-    do("v", V.tensor_tensor_scan, ("nrow",), "erow", end, T.nrow[:], T.nrow[:], 0.0, A.add, A.max)
+    do("v", V.tensor_copy, ("ct",), "cu", T.cu[:], T.ct[:])
+    do("v", V.tensor_copy, ("cu", "t8"), "nrow", T.nrow[:], T.t8[:].indirect(T.cu[:]))
+    act(("cu", "t8"), "nz", T.nz[:], T.t8[:].indirect(T.cu[:]), F.Sign)
+    scan(("nrow", "er0"), "erow", T.erow[:, 1:C + 1], T.nrow[:], T.nrow[:], 0.0, A.add, A.max)
+    scan(("nz",), "zrow", T.zrow[:], T.nz[:], T.nz[:], 0.0, A.add, A.max)
+    do("v", V.tensor_copy, ("erow",), "tot", T.msg[:, mo:mo + 1], T.erow[:, C:C + 1])
+    kcol = T.zrow[:, C - 1:C]
 
-    nls = 0
-    need("g", "erow")
-    chip, chipy = part(topo.engines(core, me["X"]), 0, 2), part(topo.engines(core, me["Y"]), 1, 2)
-    dr, hop = me["direct"], me["hop"]
+    relay = [(c, part(topo.engines(core, c), 1 - i, 2), q) for i, (c, q) in enumerate(me["relay"])]
+    nb = [x for x in relay if x[2] in me["hop"]]
+    dr = me["direct"]
 
     def direct_engines(k):
         return part(topo.engines(core, T.cores[dr[k]]), k, len(dr))
-    nls += send([(me["X"], chip, T.r1b[:], mine)], "r1")
-    nls += send([(T.cores[q], direct_engines(k), T.tot[:, 4 * r:4 * r + 1], mine) for k, q in enumerate(dr)], "m1_%d" % r)
+    need("g", "tot")
+    nls = send([(c, es, T.r1b[:, 0:1], T.msg[:, mo:mo + 1], "r1") for c, es, q in relay])
 
-    do("v", V.tensor_tensor_scan, ("erow", "er0", "dg"), "se", T.se[:], T.erow[:, 7:135], T.dg[:, 0:128], BIG, A.min, A.max)
-    do("v", V.tensor_tensor_scan, ("nz",), "zrow", T.zrow[:], T.nz[:], T.nz[:], 0.0, A.add, A.max)
-    act(("erow",), "tot", T.tot[:, 4 * r:4 * r + 1], mine, F.Copy)
-    kt, ktk = T.c5h, "c5h"
-    if up:
-        act(("c5h", "erow"), "kt5", T.kt5[:, 0:5], T.c5h[:, 0:5], bias=mine)
-        kt, ktk = T.kt5, "kt5"
-    for c in range(8):
-        act(("zrow", "k8"), "acc", T.junk[:, 128 * c:128 * c + 127], T.zrow[:, 0:127], F.Sign,
-            bias=T.k8[:, c:c + 1], scale=-1.0, accum_out=T.acc[:, c:c + 1])
-    do("v", V.tensor_tensor, ("se",), "et", T.et[:, 1:9], T.se[:, 14:128:16], T.se[:, 15:128:16], A.min)
-    do("v", V.tensor_tensor, ("et", "et0"), "de", T.de[:], T.et[:, 1:9], T.et[:, 0:8], A.subtract)
-    do("v", V.tensor_tensor, ("de", "fl8"), "vv", T.vv[:], T.de[:], T.fl8[:], A.add)
-    do("v", V.tensor_tensor_scan, ("vv", "pw"), "pkf", T.pkf[:], T.pw[:], T.vv[:], 0.0, A.mult, A.add)
-    do("v", V.tensor_copy, ("pkf",), "pk", T.pk[:], T.pkf[:, 1:8:2])
-
-    need("g", "pk")
-    nls += send([(me["Y"], chipy, T.r2b[:], T.pk[:])], "r2")
-    nls += send([(T.cores[q], direct_engines(k), T.l2[:, 4 * (r - first(q)):4 * (r - first(q)) + 4], T.pk[:])
-                 for k, q in enumerate(dr)], "m2")
-    o = 4 * (r - fi)
-    dma("y", ("pk",), "l2own", "l2d", T.l2[:, o:o + 4], T.pk[:])
-
-    do("v", V.quantize_mx, ("xb",), "xq", T.xq[:], T.xs[:], T.xb[:])
-    do("v", V.memset, (), "mr0", T.mr2[:, SH:SH + P], 0.0)
-    do("v", V.tensor_scalar, ("fm", "paf"), "dg2", T.dg[:, 128:256], T.fm[:, 1:129], paf, BIG, A.is_equal, A.mult)
-    do("v", V.tensor_scalar, ("acc",), "comp", T.comp[:], T.acc[:], 0.5, 63.5, A.mult, A.add)
-    for k in range(2):
-        do("v", V.memset, (), "slots", T.slots[:, C * k:C * k + C], float(OFF + DS * k))
-    do("v", V.tensor_copy, ("xq", "comp"), "xc", T.xc[:, 0:C].bitcast(dt.uint32), T.xq[:].bitcast(dt.uint32).indirect(T.comp[:, 0:8]))
-    act(("erow", "comp"), "ce", T.ce[:], end.indirect(T.comp[:, 0:8]), F.Copy)
-    act(("xq", "comp"), "xcs", T.xcs[:, 0:C], T.xs[:].indirect(T.comp[:, 0:8]), F.Copy)
-    for k in range(2, n):
-        do("v", V.memset, (), "slots", T.slots[:, C * k:C * k + C], float(OFF + DS * k))
-    do("v", V.quantize_mx, ("wb",), "wq", T.wq[:], T.ws[:], T.wb[:])
-    dma("y", ("xq",), "xpad", "pad", codes(T.xc[:, C:C + DS]), codes(T.xq[:, 0:DS]))
-    dma("y", ("xq",), "xpad", "pad", T.xcs[:, C:C + DS], T.xs[:, 0:DS])
-
-    iota("ikh", [[16, 8]])
-    iota("prz", [[0, 40]], 0, T.prx[:])
-    if r < 3:
-        iota("pr0", [[0, 1]], SH - r * P, T.prx[:, 0:1], reads=("prz",))
-    iota("fm8", [[0, 5], [1, 8]])
-    iota("idump", [[16, 40]], DUMP)
-    act(("paf",), "paf2", one["paf2"], paf, scale=2.0, bias=127.0)
-    act(("ikh", "paf2"), "ik2", T.ik2[:], T.ikh[:], scale=2.0, bias=one["paf2"])
-    for i, q in enumerate(hop):
-        d = q - (r - 2)
-        act(("ce", ktk), "nce", T.nce[:, C * i:C * i + 127], T.ce[:, 0:127], scale=-1.0, bias=kt[:, d:d + 1])
-    act(("fm8",), "rst8", T.rst8[:], T.fm8[:], F.Sign)
-    act(("idump", "paf"), "di", T.di[:], T.idump[:], bias=paf)
-
-    n2, nd = 0, 0
-    for s in range(N):
-        for kind in ("hop1", "direct"):
-            if r in pl[s][kind]:
-                ev["m1_%d" % s] = ("m1_%d" % s, 8 // len(pl[s][kind]))
-        if r in pl[s]["hop"]:
-            n2 += 8 // len(pl[s]["hop"])
-            nd += 8
-        elif r in pl[s]["direct"]:
-            n2 += 8 // len(pl[s]["direct"])
-            nd += 8 // len(pl[s]["direct"])
-    ev["m2"], ev["dc"], ev["dsc"] = ("m2", n2), ("dc", nd), ("dsc", nd)
-
-    ns = needs(r)
-    if ns:
-        act(["m1_%d" % s for s in ns], "sg", T.junp[:, 8:8 + len(ns)], T.tot[:, 4 * ns[0]:4 * ns[-1] + 1:4], F.Copy,
-            scale=1.0 if up else -1.0, accum_out=one["sg"])
-
-    if r == 3:
-        do("v", V.tensor_scalar, ("prz", "m1_0"), "pr0", T.prx[:, 0:1], T.tot[:, 0:1], float(SH - r * P), None, A.add)
-    elif up:
-        do("v", V.tensor_reduce, ["m1_%d" % s for s in range(fi, N) if s != r] + ["tot"], "pa", one["pa"],
-           T.tot[:, 4 * fi:4 * (N - 1) + 1:4], X, A.add)
-        do("v", V.tensor_scalar, ("prz", "pa"), "pr0", T.prx[:, 0:1], one["pa"], -1.0, float(SH + (N - r) * P), A.mult, A.add)
-    steps = T.tot[:, 4 * fi:4 * (hi - 1) + 1:4]
-    do("v", V.tensor_tensor_scan, ["m1_%d" % s for s in range(fi, hi) if s != r] + ["tot", "pr0", "prz"], "prx",
-       T.prx[:, 8:8 * (n - 1) + 1:8], steps, steps, T.prx[:, 0:1], A.add, A.max)
-
-    for i, q in enumerate(hop):
-        d = q - (r - 2)
-        row = T.nce[:, C * i:C * i + 127]
-        if ns:
-            act(("nce", "sg"), "a%d" % d, T.junl[:, C * d:C * d + 127], row, F.Sign, bias=one["sg"], accum_out=one["a%d" % d])
+    thr, tk = T.k8, "k8"
+    if up(r):
+        act(("k8", "zrow"), "k8k", T.k8k[:, 0:4], T.k8[:, 0:4], bias=kcol)
+        thr, tk = T.k8k, "k8k"
+    for c in range(4):
+        act(("zrow", tk), "acc", T.junk[:, C * c:C * c + C - 1], T.zrow[:, 0:C - 1], F.Sign,
+            bias=thr[:, c:c + 1], scale=-1.0, accum_out=T.acc[:, c:c + 1])
+        o, k = T.cmp[:, C * c + 1:C * c + C], T.k8b[:, 4 + c:5 + c]
+        if up(r):
+            ts(("zrow", "k8b"), "cmp", o, T.zrow[:, 0:C - 1], kcol, k, A.subtract, A.is_le)
         else:
-            act(("nce",), "a%d" % d, T.junl[:, C * d:C * d + 127], row, F.Sign, accum_out=one["a%d" % d])
-    thr, tk = kt, ktk
-    if ns:
-        act((ktk, "sg"), "thr", T.thr[:, 0:5], kt[:, 0:5], bias=one["sg"])
-        thr, tk = T.thr, "thr"
+            ts(("zrow", "k8b"), "cmp", o, T.zrow[:, 0:C - 1], k, None, A.is_le)
+    scan(("cmp", "cmp0", "rm"), "cs", T.cs[:], T.rm[:], T.cmp[:], 0.0, A.mult, A.add)
+    do("v", V.quantize_mx, ("xb",), "xq", T.xq[:], T.xs[:], T.xb[:])
+    do("v", V.tensor_copy, ("cs",), "comp1", T.comp[:, 4:8], T.cs[:, C - 1:4 * C:C])
+    ts(("acc",), "comp", T.comp[:, 0:4], T.acc[:], 0.5, (C - 1) / 2.0, A.mult, A.add)
+    if up(r):
+        ts(("t32", "zrow"), "fl", T.fl[:], T.t32[:], kcol, float(C), A.add, A.is_lt)
+    else:
+        ts(("t32", "zrow"), "fl", T.fl[:], T.t32[:], kcol, None, A.is_ge)
 
-    def counts(dsts):
-        for q in dsts:
-            d = q - (r - 2)
-            act(("ce", tk), "a%d" % d, T.junl[:, C * d:C * d + 127], T.ce[:, 0:127], F.Sign,
-                bias=thr[:, d:d + 1], scale=-1.0, accum_out=one["a%d" % d])
+    act(("erow", "comp"), "ce", T.ce[:], T.erow[:, 0:C].indirect(T.comp[:]), F.Copy)
+    pick((("xq", "comp"), ("xq", "comp")), "x", T.xc[:], T.xcs[:], T.xq[:], T.xs[:], T.comp[:])
+    tt(("fl", "di"), "dmp", T.dmp[:], T.fl[:], T.di[:], A.mult)
+    do("v", V.transpose, ("ce",), "cet", T.cet[:], T.ce[:])
+    ts(("zrow",), "mm", one["mm"], kcol, float(DS), None, A.max)
+    tt(("cet", "dmp"), "pf", T.pf[:], T.cet[:, 0:C:32], T.dmp[:], A.add)
+    ts(("zrow",), "mu", T.msg[:, mo + 1:mo + 2], kcol, float(DS), None, A.max)
+    do("v", V.tensor_copy, ("pf",), "beg", T.msg[:, mo + 2:mo + 6], T.pf[:])
 
-    def lists(dsts, lf, name):
-        for i, q in enumerate(dsts):
-            d = q - (r - 2)
-            act(("ik2", "a%d" % d), name + "f", lf[:, 5 * i:5 * i + 5], T.ik2[:, 0:5], bias=one["a%d" % d])
+    need("g", "beg")
+    nls += send([(c, es, T.r2b[:], T.msg[:, mo + 2:mo + 6], "r2") for c, es, q in nb])
+    nls += send([(T.cores[q], direct_engines(k), T.msg[:, block(r, q):block(r, q) + 6], T.msg[:, mo:mo + 6], "md")
+                 for k, q in enumerate(dr)])
+    nls += send([(c, es, codes(T.rcb[:]), codes(T.xc[:]), "rc") for c, es, q in nb])
+    need("g", "xs")
+    nls += send([(c, es, T.rsb[:], T.xcs[:], "rsc") for c, es, q in nb])
+    b = lay[r]
+    dma("y", ("xc",), "own", "own", codes(win[:, b:b + C]), codes(T.xc[:]))
+    dma("y", ("xs",), "own", "own", wins[:, b:b + C], T.xcs[:])
 
-    def clamp(k, lf, ls, name):
-        do("v", V.tensor_scalar, (name + "f",), name, ls[:, 0:5 * k], lf[:, 0:5 * k], 0.5, 127.0, A.mult, A.min)
+    def columns(items):
+        tot = 0
+        for i in (0, 1):
+            need("g", *[x[3][i] for x in items])
+            tr = []
+            for k, x in enumerate(items):
+                q = x[0]
+                o = window(T, q)[i][:, layout(q)[r]:layout(q)[r] + DS]
+                es = part(topo.engines(core, T.cores[q]), k, len(items))
+                tr.append((T.cores[q], es, o, x[2], "sd") if i else (T.cores[q], es, codes(o), codes(x[1]), "cd"))
+            tot += send(tr)
+        return tot
 
-    def pick(k, dst, ls, name, *keys):
-        do("v", V.tensor_copy, ("xc", name) + keys, name + "c", dst.bitcast(dt.uint32),
-           T.xc[:, 0:C + DS * len(keys)].bitcast(dt.uint32).indirect(ls[:, 0:5 * k]))
+    j80 = T.j16[:, 0:5]
+    if mid(r):
+        if up(r):
+            ts(("j16", "mm"), "l80", T.l80[:, 0:5], j80, one["mm"], float(C), A.subtract, A.add)
+        else:
+            ts(("j16", "mm"), "l80", T.l80[:, 0:5], j80, one["mm"], float(DS), A.add, A.subtract)
+        pick((("xc", "l80"), ("xs", "l80")), "sp", T.sp[:], T.sps[:], T.xc[:], T.xcs[:], T.l80[:, 0:5])
+        nls += columns([(q, T.xc[:, ends(r)], T.xcs[:, ends(r)], ("xc", "xs")) if (q > r) == up(r) else
+                        (q, T.sp[:], T.sps[:], ("spc", "sps")) for q in dr])
+    else:
+        nbr = r - 1 if up(r) else r + 1
+        both = slice(lay[min(r, nbr)], lay[min(r, nbr)] + 2 * C)
+        other = REST - DS if up(r) else C + DS
+        if up(r):
+            act(("mm",), "dl", one["dl"], one["mm"], scale=-1.0, bias=float(2 * C - other))
+        else:
+            act(("mm",), "dl", one["dl"], one["mm"], bias=float(-DS - other))
+        act(("j16",), "j80", T.j80[:, 0:5], j80, bias=float(other))
 
-    def picks(k, dst, ls, name, *keys):
-        act(("xcs", name) + keys, name + "s", dst, T.xcs[:, 0:C + DS * len(keys)].indirect(ls[:, 0:5 * k]), F.Copy)
-    ka, kb = len(hop), len(dr)
-    counts(dr[:1])
-    for i, q in enumerate(hop):
-        a = "a%d" % (q - (r - 2))
-        do("v", V.tensor_scalar, ("ik2", a), "la", T.lsa[:, 5 * i:5 * i + 5], T.ik2[:, 0:5], one[a], 0.5, A.add, A.mult)
-    pick(ka, T.spa[:, 0:DS * ka], T.lsa, "la", "xpad")
-    picks(ka, T.spas[:, 0:DS * ka], T.lsa, "la", "xpad")
-    relay = [(me["X"], chip), (me["Y"], chipy)]
-    need("g", "lac")
-    nls += send([(c, es, codes(T.rcb[:]), codes(T.spa[:, DS * i:DS * i + DS])) for i, (c, es) in enumerate(relay[:ka])], "rc")
-    need("g", "las")
-    nls += send([(c, es, T.rsb[:], T.spas[:, DS * i:DS * i + DS]) for i, (c, es) in enumerate(relay[:ka])], "rsc")
-    counts(dr[1:])
-    lists(dr, T.lfb, "lb")
-    counts([r])
-    lists([r], T.lfo, "lo")
-    act(("prx",), "ia", T.junp[:, 0:n - 1], T.prx[:, 8:8 * (n - 1) + 1:8], F.Sign, scale=-1.0, bias=SH + 0.5, accum_out=one["ia"])
+    ts(("fm", "paf"), "dg", T.dg[:], T.fm[:], one["paf"], BIG, A.is_equal, A.mult)
+    act(("i64", "h16"), "t64", T.t64[:], T.i64[:], bias=one["h16"])
+    do("v", V.quantize_mx, ("wb",), "wq", T.wq[:], T.ws[:], T.wb[:])
 
-    do("v", V.tensor_copy, ("m2", "l2own"), "wi", T.wi[:, 0:4 * n], T.l2[:, 0:4 * n])
-    wi = T.wi[:, 0:4 * n]
-    do("v", V.tensor_scalar, ("wi",), "dei", T.dei[:, 1:m:2], wi, 127, None, A.bitwise_and)
-    do("v", V.tensor_scalar, ("wi",), "dei2", T.dei[:, 0:m:2], wi, 8, 127, A.logical_shift_right, A.bitwise_and)
-    do("v", V.tensor_scalar, ("wi",), "fli", T.fli[:, 1:m:2], wi, 7, 1, A.logical_shift_right, A.bitwise_and)
-    do("v", V.tensor_scalar, ("wi",), "fli2", T.fli[:, 0:m:2], wi, 15, None, A.logical_shift_right)
-    do("v", V.tensor_tensor, ("dei2", "prx"), "def_", T.def_[:, 0:m], T.dei[:, 0:m], T.prx[:, 0:m], A.add)
-    do("v", V.tensor_tensor, ("fli2", "di"), "fd", T.fd[:, 0:m], T.fli[:, 0:m], T.di[:, 0:m], A.mult)
-    clamp(kb, T.lfb, T.lsb, "lb")
-    do("v", V.tensor_tensor_scan, ("def_", "rst8"), "er", T.er[:, 0:m], T.rst8[:, 0:m], T.def_[:, 0:m], 0.0, A.mult, A.add)
-    pick(kb, T.spb[:, 0:DS * kb], T.lsb, "lb")
-    picks(kb, T.spbs[:, 0:DS * kb], T.lsb, "lb")
-    need("g", "lbc")
-    nls += send([(T.cores[q], direct_engines(i), codes(T.win[:, base(r, q):base(r, q) + DS]), codes(T.spb[:, DS * i:DS * i + DS]))
-                 for i, q in enumerate(dr)], "dc")
-    need("g", "lbs")
-    nls += send([(T.cores[q], direct_engines(i), T.wins[:, base(r, q):base(r, q) + DS], T.spbs[:, DS * i:DS * i + DS])
-                 for i, q in enumerate(dr)], "dsc")
-    do("v", V.tensor_tensor, ("er", "fd"), "po", T.po[:, 0:m], T.er[:, 0:m], T.fd[:, 0:m], A.add)
-    clamp(1, T.lfo, T.lso, "lo")
-    do("v", V.tensor_copy, ("po",), "pos", T.pos[:, 0:m], T.po[:, 0:m])
-    act(("ia",), "g0", T.g[:, 0:1], one["ia"], scale=DS / 2.0, bias=float(OFF + DS * (n - 1) // 2))
+    got = {"m1": 0, "m2": 0, "md": 0, "cd": 0, "sd": 0}
+    for s in range(N):
+        for c, q in pl[s]["relay"]:
+            if q == r:
+                e = len(topo.engines(c, core))
+                got["m1"] += e
+                if abs(s - r) == 1:
+                    got["m2"] += e
+                    got["c1" if s < r else "c2"] = got["s1" if s < r else "s2"] = e
+        if r in pl[s]["direct"]:
+            e = len(topo.engines(T.cores[s], core)) // len(pl[s]["direct"])
+            for k in ("md", "cd", "sd"):
+                got[k] += e
+    for k, v in got.items():
+        ev[k] = (k, v)
 
-    do("v", V.tensor_copy, ("pos", "slots", "mr0"), "mr2", T.mr2[:].indirect(T.pos[:, 0:m]), T.slots[:, 0:16 * m])
-    b = base(r, r)
-    pick(1, T.win[:, b:b + DS], T.lso, "lo")
-    picks(1, T.wins[:, b:b + DS], T.lso, "lo")
-    do("v", V.tensor_scalar, ("mr2",), "mk", T.mk[:], T.mr2[:, SH:SH + P], 0.0, None, A.is_gt)
-    do("v", V.tensor_tensor_scan, ("mk", "g0"), "g", T.g[:, 1:P], T.mk[:, 1:P], T.mr2[:, SH + 1:SH + P], T.g[:, 0:1], A.add, A.max)
-    do("v", V.tensor_tensor_scan, ("g", "dg2"), "sgm", T.sgm[:], T.g[:], T.dg[:], BIG, A.min, A.max)
-    do("v", V.tensor_tensor, ("sgm",), "mn", T.mn[:], T.sgm[:, 14:256:16], T.sgm[:, 15:256:16], A.min)
-    do("v", V.tensor_copy, ("mn",), "fin", T.fin[:], T.mn[:])
+    def values(i, reads, bias):
+        act(("t64",) + reads, "val%d" % i, T.val[:, 64 * i:64 * i + 64], T.t64[:], bias=bias)
+    later = []
+    for i, s in enumerate(src):
+        if mid(r) and s == short(r)[0]:
+            later.append(i)
+        elif abs(s - r) < 2:
+            values(i, (), float(lay[s]))
+        elif (r > s) == up(s):
+            values(i, (), float(lay[s] - ends(s).start))
+        else:
+            mu, k = T.msg[:, block(s, r) + 1:block(s, r) + 2], "b%d" % i
+            if up(s):
+                ts(("md",), k, one[k], mu, float(lay[s] - C), None, A.add)
+            else:
+                ts(("md",), k, one[k], mu, -1.0, float(lay[s] + DS), A.mult, A.add)
+            if mid(r) and s == short(r)[1] and not up(r):
+                later.append(i)
+            else:
+                values(i, (k,), one[k])
 
+    m = len(needs(r))
+    do("v", V.tensor_copy, ("m1", "md", "tot"), "tf", T.tf[:, 0:m], T.msg[:, 0:8 * (m - 1) + 1:8])
+    scan(("tf", "zer"), "sc", T.sc[:, 0:m], T.zer[:, 0:m], T.tf[:, 0:m], float(SH + (N * up(r) - r) * P), A.add,
+         A.subtract if up(r) else A.add)
+
+    def shift(s):
+        j = N - 1 - s if up(r) else s - 1
+        return T.sc[:, j:j + 1] if j >= 0 else float(SH - r * P)
+
+    def begins(i):
+        s = src[i]
+        o = block(s, r)
+        ts(("sc", "beg" if s == r else "m2" if abs(s - r) == 1 else "md"), "pos", T.pos[:, 4 * i:4 * i + 4],
+           T.msg[:, o + 2:o + 6], shift(s), None, A.add)
+
+    if mid(r):
+        a, z = short(r)
+        ia, iz = src.index(a), src.index(z)
+        if up(r):
+            act(("sc",), "sg", one["sg"], shift(z), F.Sign, scale=-1.0, bias=SH + P - 0.5)
+        else:
+            act(("sc",), "sg", one["sg"], shift(a), F.Sign, bias=-(SH + 0.5))
+        act(("sg",), "ba", one["ba"], one["sg"], scale=(lay[a] - lay["dup"]) / 2.0,
+            bias=(lay[a] + lay["dup"]) / 2.0 - ends(a).start)
+        if iz in later:
+            act(("sg", "b%d" % iz), "bb", one["bb"], one["sg"], F.Relu, scale=-float(WIN))
+        values(ia, ("ba",), one["ba"])
+        if iz in later:
+            act(("bb",), "bb2", one["dv"], one["bb"], scale=-1.0, bias=one["b%d" % iz])
+            values(iz, ("bb2",), one["dv"])
+        side = "2" if up(r) else "1"
+        dma("y", ("c" + side,), "dup", "dup", codes(win[:, lay["dup"]:lay["dup"] + DS]), codes(win[:, lay[a]:lay[a] + DS]))
+        dma("y", ("s" + side,), "dup", "dup", wins[:, lay["dup"]:lay["dup"] + DS], wins[:, lay[a]:lay[a] + DS])
+    else:
+        if up(r):
+            ts(("sc", "dl"), "dv", one["dv"], shift(r), SH - P - 0.5, one["dl"], A.is_lt, A.mult)
+        else:
+            ts(("sc", "dl"), "dv", one["dv"], shift(r + 1), SH + 2 * P + 0.5, one["dl"], A.is_gt, A.mult)
+    for i, s in enumerate(src):
+        if abs(s - r) != 1:
+            begins(i)
+    if not mid(r):
+        if up(r):
+            ts(("j80", "dv"), "l80", T.l80[:, 0:5], T.j80[:, 0:5], one["dv"], 0.0, A.add, A.max)
+        else:
+            ts(("j80", "dv"), "l80", T.l80[:, 0:5], T.j80[:, 0:5], one["dv"], float(2 * C - 1), A.add, A.min)
+    for i, s in enumerate(src):
+        if abs(s - r) == 1:
+            begins(i)
+
+    if not mid(r):
+        side = "1" if up(r) else "2"
+        pick((("l80", "own", "c" + side), ("l80", "own", "s" + side)), "late", T.late[:], T.lates[:],
+             win[:, both], wins[:, both], T.l80[:, 0:5])
+        nls += columns([(dr[0], T.late[:], T.lates[:], ("latec", "lates"))])
+
+    do("v", V.tensor_copy, ["pos", "tab0"] + ["val%d" % i for i in range(n)], "tab", T.tab[:].indirect(T.pos[:, 0:4 * n]), T.val[:, 0:64 * n])
+    seg = T.tab[:, SH - BACK:SH + P]
+    scan(("tab",), "run", T.run[:, 0:P + BACK], seg, seg, 0.0, A.max, A.max)
+    scan(("run", "dg"), "held", T.held[:, 0:P], T.dg[:], T.run[:, BACK:BACK + P], 0.0, A.add, A.min)
+    do("v", V.transpose, ("held", "held0"), "ya", T.ya[:], T.held[:, 15:2 * P:16])
+    for h in (0, 1):
+        tt(("ya",), "yb", T.yb[:, 16 * h:16 * h + 16], T.ya[:, 0:16], T.ya[:, 16:32], A.max)
+    do("v", V.transpose, ("yb",), "yc", T.yc[:], T.yb[:])
+    do("v", V.tensor_copy, ("yc",), "fin", T.fin[:], T.yc[:, 0:16])
+
+    wc = ["fin", "own", "cd"] + [k for k in ("c1", "c2", "dup") if k in ev]
+    wsc = ["fin", "own", "sd"] + [k for k in ("s1", "s2", "dup") if k in ev]
     for b in (0, 1):
-        do("v", V.tensor_copy, ("dc", "loc", "fin"), "t%d" % b, T.t2[:, 128 * b:128 * b + 128].bitcast(dt.uint32),
-           T.win[:].bitcast(dt.uint32).indirect(T.fin[:, 8 * b:8 * b + 8]))
-        act(("dsc", "los", "fin"), "t%ds" % b, T.t2s[:, 128 * b:128 * b + 128],
-            T.wins[:].indirect(T.fin[:, 8 * b:8 * b + 8]), F.Copy)
+        pick((wc, wsc), "t%d" % b, T.t2[:, C * b:C * b + C], T.t2s[:, C * b:C * b + C], win[:], wins[:], T.fin[:, 8 * b:8 * b + 8])
     for b in (0, 1):
         for o in (0, 1):
             k = 2 * b + o
-            do("t", g.tensor.matmul_mx, ("wq", "t%d" % b, "t%ds" % b), "mm%d" % k, T.ps[:, 512 * k:512 * k + 128],
-               T.wq[:, 128 * k:128 * k + 128], T.ws[:, 128 * k:128 * k + 128],
-               T.t2[:, 128 * b:128 * b + 128], T.t2s[:, 128 * b:128 * b + 128], True, True)
+            do("t", g.tensor.matmul_mx, ("wq", "t%dc" % b, "t%ds" % b), "mm%d" % k, T.ps[:, 512 * k:512 * k + C],
+               T.wq[:, C * k:C * k + C], T.ws[:, C * k:C * k + C], T.t2[:, C * b:C * b + C], T.t2s[:, C * b:C * b + C], True, True)
     for b in (0, 1):
-        do("v", V.tensor_copy, ("mm%d" % (2 * b),), "y0", T.ysb[:, 128 * b:128 * b + 128], T.ps[:, 1024 * b:1024 * b + 128])
-        act(("mm%d" % (2 * b + 1),), "y1", T.ysb[:, P + 128 * b:P + 128 * b + 128], T.ps[:, 1024 * b + 512:1024 * b + 640], F.Copy)
-    dma("y", ("y0", "y1"), "st0", "st0", T.y[:], T.ysb[:])
+        lo, hi = slice(C * b, C * b + C), slice(P + C * b, P + C * b + C)
+        do("v", V.tensor_copy, ("mm%d" % (2 * b),), "y0", T.ysb[:, lo], T.ps[:, 1024 * b:1024 * b + C])
+        dma("y", ("y0",), "st", "st", T.y[:, lo], T.ysb[:, lo])
+        act(("mm%d" % (2 * b + 1),), "y1", T.ysb[:, hi], T.ps[:, 1024 * b + 512:1024 * b + 512 + C], F.Copy)
+        dma("s", ("y1",), "st", "st", T.y[:, hi], T.ysb[:, hi])
 
     for q, s in own.items():
         ev["end_" + q] = (s, count[q])
     for s, v in final.items():
         ev["end_" + s] = (s, v)
     ev["end_ls"] = ("ls", nls)
-    need("g", *[k for k in ev if k.startswith("end_") or k.startswith("m1_")], "m2", "dc", "dsc")
+    need("g", *[k for k in ev if k.startswith("end_")], *got)

@@ -3,14 +3,14 @@ from concourse.mybir import dt, AluOpType as A, ActivationFunctionType as F
 
 N, C, P, DS = 8, 128, 256, 80
 REST = C - DS
-WIN = 4 * DS + 2 * C
+WIN = 512
 BACK = 5
 SH = 4 * P + 16
 DUMP = SH + 5 * P + 16
 TAB = 2 * DUMP + N * C
 BIG = 1.0e6
 
-f32, bf, i32, u16, u8, c4 = "float32", "bfloat16", "int32", "uint16", "uint8", "float8_e4m3fn_x4"
+f32, bf, f16, i32, u16, u8, c4 = "float32", "bfloat16", "float16", "int32", "uint16", "uint8", "float8_e4m3fn_x4"
 SCRATCH = {}
 for _n, _w, _d in [
     ("one", 32, f32), ("onei", 8, i32),
@@ -19,20 +19,20 @@ for _n, _w, _d in [
     ("i64", 64, f32), ("t64", 64, f32), ("fm", P, bf), ("dg", P, bf),
     ("nrow", C, bf), ("nz", C, bf), ("erow", C + 8, f32), ("zrow", C, bf),
     ("junk", 4 * C, f32), ("acc", 4, f32), ("rm", 4 * C, bf), ("cmp", 4 * C, bf), ("cs", 4 * C, bf), ("comp", 8, u16),
-    ("ce", C, f32), ("cet", C, f32), ("msg", 8 * N, u16), ("tf", 8, f32), ("zer", 8, f32), ("sc", 8, f32),
-    ("l80", 6, u16), ("pos", 20, u16), ("val", 5 * 64, f32), ("tab", TAB, f32), ("run", P + 8, f32), ("held", 2 * P, f32),
-    ("ya", 32, f32), ("yb", 32, f32), ("yc", 32, f32), ("fin", 16, u16),
+    ("ce", C, f32), ("cet", C, f32), ("msg", 8 * N, u16), ("tf", 8 * N, f16), ("zer", 8, f32), ("sc", 8, f32),
+    ("l80", 6, u16), ("pos", 20, u16), ("val", 5 * 64, f32), ("tab", TAB, f32), ("run", P + 8, f16), ("held", 2 * P, f16),
+    ("ya", 32, f16), ("yb", 32, i32), ("yc", 32, i32), ("yd", 16, i32), ("fin", 16, u16),
     ("xb", 512, bf), ("xq", C, c4), ("xs", C, u8), ("xc", C, c4), ("xcs", C, u8),
     ("sp", DS, c4), ("sps", DS, u8), ("late", DS, c4), ("lates", DS, u8),
     ("wine", WIN, c4), ("wines", WIN, u8), ("winm", WIN, c4), ("winms", WIN, u8), ("t2", P, c4), ("t2s", P, u8),
     ("wb", 2048, bf), ("wq", 512, c4), ("ws", 512, u8), ("ysb", 512, f32),
-    ("r1b", 2, u16), ("r2b", 4, u16), ("rcb", C, c4), ("rsb", C, u8),
+    ("r1b", 2, f16), ("r2b", 4, u16), ("rcb", C, c4), ("rsb", C, u8),
 ]:
     SCRATCH[_n] = ("sbuf", [128, _w], _d)
-ONE = {k: i for i, k in enumerate(["paf", "puf", "h16", "paf5", "mm", "dl", "dv", "sg", "ba", "bb", "b0", "b1", "b2", "b3", "b4"])}
+ONE = {k: i for i, k in enumerate(["paf", "puf", "h16", "paf5", "sum", "mm", "dl", "dv", "b0", "b1", "b2", "b3", "b4"])}
 ONEI = {k: i for i, k in enumerate(["ip", "ipa", "ipu"])}
 SCRATCH["ps"] = ("psum", [128, 2048], f32)
-SEMAPHORES = ["cl", "xl", "wl", "own", "dup", "vs", "ss", "ts", "gs", "ls", "m1", "m2", "md", "cd", "sd",
+SEMAPHORES = ["cl", "xl", "wl", "vs", "ss", "ts", "gs", "ls", "m1", "m2", "md", "cd", "sd",
               "c1", "s1", "c2", "s2", "r1", "r2", "rc", "rsc", "st"]
 
 
@@ -58,16 +58,22 @@ def short(q):
 
 def layout(q):
     out, at = {}, 0
-    if mid(q) and not up(q):
-        out["dup"], at = 0, DS
     if not mid(q) and up(q):
         at = -DS % 32
     for s in sources(q):
-        out[s] = at
-        at += DS if abs(s - q) == 2 or (mid(q) and s == short(q)[0]) else C
-    if mid(q) and up(q):
-        out["dup"] = at
+        if mid(q) and s == short(q)[0]:
+            at = at + DS if up(q) else WIN - DS
+            out[s] = at
+            at = at + WIN - DS if up(q) else WIN + DS
+        else:
+            out[s] = at
+            at += DS if abs(s - q) == 2 else C
     return out
+
+
+def slot(s, q, w):
+    b = layout(q)[s] % WIN
+    return slice(b, b + w)
 
 
 def block(s, q):
@@ -83,11 +89,23 @@ def plan(T, topo):
         direct = [q for q in near if topo.may_write(core, T.cores[q])]
         hop = [q for q in near if q not in direct]
         relays = [c for c in topo.cores_of(core) if c != core and all(topo.may_write(c, T.cores[q]) for q in hop + far)]
-        X = [c for c in relays if topo.die(c) == topo.die(core)][0]
-        Y = [c for c in relays if topo.die(c) != topo.die(core)][0]
-        dst = (hop[::-1] if up(r) else hop) + far
-        out.append({"direct": direct, "hop": hop, "relay": list(zip((X, Y), dst))})
+        X = [c for c in relays if topo.die(c) == topo.die(core)]
+        Y = [c for c in relays if topo.die(c) != topo.die(core)]
+        a, b = (hop[::-1] if up(r) else hop) + far
+        if far:
+            X, Y = Y, X
+        jobs = {X[0]: [("r1", a), ("r2", a), ("rc", a)], X[1]: [("rsc", a)], Y[0]: [("r1", b)]}
+        if not far:
+            jobs[Y[0]] += [("r2", b), ("rc", b)]
+            jobs[Y[1]] = [("rsc", b)]
+        if mid(r):
+            jobs[X[0]].append(("rc", r + 2 if up(r) else r - 2))
+            jobs[X[1]].append(("rsc", r + 2 if up(r) else r - 2))
+        out.append({"direct": direct, "jobs": jobs})
     return out
+
+
+SY = 0
 
 
 def mask_of(es):
@@ -127,23 +145,27 @@ def ends(r):
     return slice(REST, C) if up(r) else slice(0, DS)
 
 
-def relay_program(g, core, T, topo, r, q, got):
+def relay_program(g, core, T, topo, r, jobs, got):
     send = sender(g, core, T, topo)
-    dst = T.cores[q]
-    es = topo.engines(core, dst)
-    o = block(r, q)
-    g.wait_ge(T.sem["r1"], got)
-    n = send([(dst, es, T.msg[:, o:o + 1], T.r1b[:, 0:1], "m1")])
-    if abs(q - r) == 1:
+    n, seen = 0, set()
+    for what, q in jobs:
+        dst = T.cores[q]
+        o = block(r, q)
         win, wins = window(T, q)
-        cut = ends(r) if mid(q) and short(q)[0] == r else slice(0, C)
-        b, w, side = layout(q)[r], cut.stop - cut.start, "1" if r < q else "2"
-        g.wait_ge(T.sem["r2"], got)
-        n += send([(dst, es, T.msg[:, o + 2:o + 6], T.r2b[:], "m2")])
-        g.wait_ge(T.sem["rc"], got)
-        n += send([(dst, es, codes(win[:, b:b + w]), codes(T.rcb[:, cut]), "c" + side)])
-        g.wait_ge(T.sem["rsc"], got)
-        n += send([(dst, es, wins[:, b:b + w], T.rsb[:, cut], "s" + side)])
+        cut = ends(r) if abs(q - r) == 2 or (mid(q) and short(q)[0] == r) else slice(0, C)
+        side = "d" if abs(q - r) == 2 else "1" if r < q else "2"
+        if what not in seen:
+            g.wait_ge(T.sem[what], got)
+            seen.add(what)
+        if what == "r1":
+            item = (T.tf[:, o:o + 1], T.r1b[:, 0:1], "m1")
+        elif what == "r2":
+            item = (T.msg[:, o + 2:o + 6], T.r2b[:], "m2")
+        elif what == "rc":
+            item = (codes(win[:, slot(r, q, cut.stop - cut.start)]), codes(T.rcb[:, cut]), "c" + side)
+        else:
+            item = (wins[:, slot(r, q, cut.stop - cut.start)], T.rsb[:, cut], "s" + side)
+        n += send([(dst, topo.engines(core, dst)) + item])
     g.wait_ge(T.sem["ls"], n)
 
 
@@ -152,9 +174,8 @@ def rank_program(g, core, T, topo):
     r = T.rank_of(core)
     if r is None:
         for k in range(N):
-            for c, q in pl[k]["relay"]:
-                if core == c:
-                    relay_program(g, core, T, topo, k, q, len(topo.engines(T.cores[k], c)) // 2)
+            if core in pl[k]["jobs"]:
+                relay_program(g, core, T, topo, k, pl[k]["jobs"][core], len(topo.engines(T.cores[k], core)) // 2)
         return
     me = pl[r]
     send = sender(g, core, T, topo)
@@ -235,7 +256,7 @@ def rank_program(g, core, T, topo):
     do("v", V.tensor_copy, ("ipu",), "puf", one["puf"], onei["ipu"])
     do("v", V.memset, ("rm1",), "rm", T.rm[:, 0:4 * C:C], 0.0)
     fill("cmp0", T.cmp[:, 0:4 * C:C], 0.0)
-    fill("tab0", T.tab[:, SH - BACK:SH + P], 0.0)
+    fill("tab", T.tab[:, SH - BACK:SH + P], 0.0)
     fill("zer", T.zer[:], 0.0)
     fill("held0", T.held[:, P + 15:2 * P:16], 0.0)
     act(("paf",), "paf5", one["paf5"], one["paf"], bias=0.5 - (C if up(r) else 0))
@@ -247,21 +268,23 @@ def rank_program(g, core, T, topo):
     act(("t32",), "di", T.di[:], T.t32[:], bias=float(DUMP + C * r))
 
     do("v", V.tensor_copy, ("ct",), "cu", T.cu[:], T.ct[:])
-    do("v", V.tensor_copy, ("cu", "t8"), "nrow", T.nrow[:], T.t8[:].indirect(T.cu[:]))
-    act(("cu", "t8"), "nz", T.nz[:], T.t8[:].indirect(T.cu[:]), F.Sign)
-    scan(("nrow", "er0"), "erow", T.erow[:, 1:C + 1], T.nrow[:], T.nrow[:], 0.0, A.add, A.max)
+    ts(("cu", "t8"), "nz", T.nz[:], T.t8[:].indirect(T.cu[:]), 1.0, None, A.min)
+    act(("cu", "t8"), "nrow", T.nrow[:], T.t8[:].indirect(T.cu[:]), F.Copy, accum_out=one["sum"])
     scan(("nz",), "zrow", T.zrow[:], T.nz[:], T.nz[:], 0.0, A.add, A.max)
-    do("v", V.tensor_copy, ("erow",), "tot", T.msg[:, mo:mo + 1], T.erow[:, C:C + 1])
+    do("v", V.tensor_copy, ("nrow",), "tot", T.tf[:, mo:mo + 1], one["sum"])
     kcol = T.zrow[:, C - 1:C]
 
-    relay = [(c, part(topo.engines(core, c), 1 - i, 2), q) for i, (c, q) in enumerate(me["relay"])]
-    nb = [x for x in relay if x[2] in me["hop"]]
     dr = me["direct"]
 
     def direct_engines(k):
         return part(topo.engines(core, T.cores[dr[k]]), k, len(dr))
+
+    def to_relays(what, out, in_, upper=False):
+        cs = [c for c, jobs in me["jobs"].items() if what in [k for k, q in jobs]]
+        it = [(c, part(topo.engines(core, c), 1 if upper else 1 - i, 2), out, in_, what) for i, c in enumerate(cs)]
+        return sum(send([x]) for x in it) if upper else send(it)
     need("g", "tot")
-    nls = send([(c, es, T.r1b[:, 0:1], T.msg[:, mo:mo + 1], "r1") for c, es, q in relay])
+    nls = to_relays("r1", T.r1b[:, 0:1], T.tf[:, mo:mo + 1])
 
     thr, tk = T.k8, "k8"
     if up(r):
@@ -276,33 +299,35 @@ def rank_program(g, core, T, topo):
         else:
             ts(("zrow", "k8b"), "cmp", o, T.zrow[:, 0:C - 1], k, None, A.is_le)
     scan(("cmp", "cmp0", "rm"), "cs", T.cs[:], T.rm[:], T.cmp[:], 0.0, A.mult, A.add)
-    do("v", V.quantize_mx, ("xb",), "xq", T.xq[:], T.xs[:], T.xb[:])
+    scan(("nrow", "er0"), "erow", T.erow[:, 1:C + 1], T.nrow[:], T.nrow[:], 0.0, A.add, A.max)
     do("v", V.tensor_copy, ("cs",), "comp1", T.comp[:, 4:8], T.cs[:, C - 1:4 * C:C])
     ts(("acc",), "comp", T.comp[:, 0:4], T.acc[:], 0.5, (C - 1) / 2.0, A.mult, A.add)
+
+    act(("erow", "comp"), "ce", T.ce[:], T.erow[:, 0:C].indirect(T.comp[:]), F.Copy)
     if up(r):
         ts(("t32", "zrow"), "fl", T.fl[:], T.t32[:], kcol, float(C), A.add, A.is_lt)
     else:
         ts(("t32", "zrow"), "fl", T.fl[:], T.t32[:], kcol, None, A.is_ge)
-
-    act(("erow", "comp"), "ce", T.ce[:], T.erow[:, 0:C].indirect(T.comp[:]), F.Copy)
-    pick((("xq", "comp"), ("xq", "comp")), "x", T.xc[:], T.xcs[:], T.xq[:], T.xs[:], T.comp[:])
+    do("v", V.quantize_mx, ("xb",), "xq", T.xq[:], T.xs[:], T.xb[:])
     tt(("fl", "di"), "dmp", T.dmp[:], T.fl[:], T.di[:], A.mult)
+    do("v", V.tensor_copy, ("nrow",), "tu", T.msg[:, mo:mo + 1], one["sum"])
     do("v", V.transpose, ("ce",), "cet", T.cet[:], T.ce[:])
-    ts(("zrow",), "mm", one["mm"], kcol, float(DS), None, A.max)
-    tt(("cet", "dmp"), "pf", T.pf[:], T.cet[:, 0:C:32], T.dmp[:], A.add)
     ts(("zrow",), "mu", T.msg[:, mo + 1:mo + 2], kcol, float(DS), None, A.max)
+    tt(("cet", "dmp"), "pf", T.pf[:], T.cet[:, 0:C:32], T.dmp[:], A.add)
+    ts(("zrow",), "mm", one["mm"], kcol, float(DS), None, A.max)
     do("v", V.tensor_copy, ("pf",), "beg", T.msg[:, mo + 2:mo + 6], T.pf[:])
+    mine = (win[:, slot(r, r, C)], wins[:, slot(r, r, C)])
+    xc, xcs = (T.xc[:], T.xcs[:]) if mid(r) else mine
+    pick((("xq", "comp"), ("xq", "comp")), "x", xc, xcs, T.xq[:], T.xs[:], T.comp[:])
 
     need("g", "beg")
-    nls += send([(c, es, T.r2b[:], T.msg[:, mo + 2:mo + 6], "r2") for c, es, q in nb])
+    nls += to_relays("r2", T.r2b[:], T.msg[:, mo + 2:mo + 6])
     nls += send([(T.cores[q], direct_engines(k), T.msg[:, block(r, q):block(r, q) + 6], T.msg[:, mo:mo + 6], "md")
                  for k, q in enumerate(dr)])
-    nls += send([(c, es, codes(T.rcb[:]), codes(T.xc[:]), "rc") for c, es, q in nb])
     need("g", "xs")
-    nls += send([(c, es, T.rsb[:], T.xcs[:], "rsc") for c, es, q in nb])
-    b = lay[r]
-    dma("y", ("xc",), "own", "own", codes(win[:, b:b + C]), codes(T.xc[:]))
-    dma("y", ("xs",), "own", "own", wins[:, b:b + C], T.xcs[:])
+    nls += to_relays("rsc", T.rsb[:], xcs)
+    need("g", "xc")
+    nls += to_relays("rc", codes(T.rcb[:]), codes(xc))
 
     def columns(items):
         tot = 0
@@ -311,7 +336,7 @@ def rank_program(g, core, T, topo):
             tr = []
             for k, x in enumerate(items):
                 q = x[0]
-                o = window(T, q)[i][:, layout(q)[r]:layout(q)[r] + DS]
+                o = window(T, q)[i][:, slot(r, q, DS)]
                 es = part(topo.engines(core, T.cores[q]), k, len(items))
                 tr.append((T.cores[q], es, o, x[2], "sd") if i else (T.cores[q], es, codes(o), codes(x[1]), "cd"))
             tot += send(tr)
@@ -324,8 +349,8 @@ def rank_program(g, core, T, topo):
         else:
             ts(("j16", "mm"), "l80", T.l80[:, 0:5], j80, one["mm"], float(DS), A.add, A.subtract)
         pick((("xc", "l80"), ("xs", "l80")), "sp", T.sp[:], T.sps[:], T.xc[:], T.xcs[:], T.l80[:, 0:5])
-        nls += columns([(q, T.xc[:, ends(r)], T.xcs[:, ends(r)], ("xc", "xs")) if (q > r) == up(r) else
-                        (q, T.sp[:], T.sps[:], ("spc", "sps")) for q in dr])
+        nls += columns([(r - 2 if up(r) else r + 2, T.sp[:], T.sps[:], ("spc", "sps"))])
+        pick((("xq", "comp"), ("xq", "comp")), "x", mine[0], mine[1], T.xq[:], T.xs[:], T.comp[:])
     else:
         nbr = r - 1 if up(r) else r + 1
         both = slice(lay[min(r, nbr)], lay[min(r, nbr)] + 2 * C)
@@ -342,98 +367,94 @@ def rank_program(g, core, T, topo):
 
     got = {"m1": 0, "m2": 0, "md": 0, "cd": 0, "sd": 0}
     for s in range(N):
-        for c, q in pl[s]["relay"]:
-            if q == r:
-                e = len(topo.engines(c, core))
-                got["m1"] += e
-                if abs(s - r) == 1:
-                    got["m2"] += e
-                    got["c1" if s < r else "c2"] = got["s1" if s < r else "s2"] = e
+        for c, jobs in pl[s]["jobs"].items():
+            for what, q in jobs:
+                if q == r:
+                    side = "d" if abs(s - r) == 2 else "1" if s < r else "2"
+                    k = {"r1": "m1", "r2": "m2", "rc": "c" + side, "rsc": "s" + side}[what]
+                    got[k] = got.get(k, 0) + len(topo.engines(c, core))
         if r in pl[s]["direct"]:
-            e = len(topo.engines(T.cores[s], core)) // len(pl[s]["direct"])
-            for k in ("md", "cd", "sd"):
-                got[k] += e
+            e = len(topo.engines(T.cores[s], core))
+            got["md"] += e // len(pl[s]["direct"])
+            if (r > s) != up(s):
+                got["cd"] += e
+                got["sd"] += e
     for k, v in got.items():
         ev[k] = (k, v)
 
-    def values(i, reads, bias):
-        act(("t64",) + reads, "val%d" % i, T.val[:, 64 * i:64 * i + 64], T.t64[:], bias=bias)
-    later = []
-    for i, s in enumerate(src):
-        if mid(r) and s == short(r)[0]:
-            later.append(i)
+    sets = [[s for s in src if abs(s - r) != 1]]
+    sets.append([s for s in src if s not in sets[0]])
+    cols, span, at = {}, [], 0
+    for group in sets:
+        a = at = at + at % 2
+        for s in group:
+            c = (ends(s).start // 32, ends(s).start // 32 + 3) if abs(s - r) == 2 and (r > s) == up(s) else (0, 4)
+            cols[s] = (at,) + c
+            at += c[1] - c[0]
+        span.append((a, at))
+
+    def values(s, reads, bias):
+        at, a, b = cols[s]
+        act(("t64",) + reads, "val%d" % (s in sets[1]), T.val[:, 16 * at:16 * (at + b - a)], T.t64[:, 16 * a:16 * b], bias=bias)
+    for s in sets[1] + sets[0]:
+        if (mid(r) and s == short(r)[0]) or cols[s][1:] != (0, 4):
+            values(s, (), float(lay[s] - ends(s).start))
         elif abs(s - r) < 2:
-            values(i, (), float(lay[s]))
-        elif (r > s) == up(s):
-            values(i, (), float(lay[s] - ends(s).start))
-        else:
-            mu, k = T.msg[:, block(s, r) + 1:block(s, r) + 2], "b%d" % i
+            values(s, (), float(lay[s]))
+    for s in src:
+        if abs(s - r) == 2 and cols[s][1:] == (0, 4):
+            mu, k = T.msg[:, block(s, r) + 1:block(s, r) + 2], "b%d" % (s > r)
             if up(s):
                 ts(("md",), k, one[k], mu, float(lay[s] - C), None, A.add)
             else:
                 ts(("md",), k, one[k], mu, -1.0, float(lay[s] + DS), A.mult, A.add)
-            if mid(r) and s == short(r)[1] and not up(r):
-                later.append(i)
-            else:
-                values(i, (k,), one[k])
+            values(s, (k,), one[k])
 
     m = len(needs(r))
-    do("v", V.tensor_copy, ("m1", "md", "tot"), "tf", T.tf[:, 0:m], T.msg[:, 0:8 * (m - 1) + 1:8])
-    scan(("tf", "zer"), "sc", T.sc[:, 0:m], T.zer[:, 0:m], T.tf[:, 0:m], float(SH + (N * up(r) - r) * P), A.add,
-         A.subtract if up(r) else A.add)
+    two = sorted(block(s, r) for s in dr if s in needs(r))
+    if two:
+        do("v", V.tensor_copy, ("md",), "tot", T.tf[:, two[0]:two[-1] + 1:32], T.msg[:, two[0]:two[-1] + 1:32])
+    scan(("m1", "tot", "zer"), "sc", T.sc[:, 0:m], T.zer[:, 0:m], T.tf[:, 0:8 * (m - 1) + 1:8],
+         float(SH + (N * up(r) - r) * P), A.add, A.subtract if up(r) else A.add)
 
     def shift(s):
         j = N - 1 - s if up(r) else s - 1
         return T.sc[:, j:j + 1] if j >= 0 else float(SH - r * P)
 
     def begins(i):
-        s = src[i]
-        o = block(s, r)
-        ts(("sc", "beg" if s == r else "m2" if abs(s - r) == 1 else "md"), "pos", T.pos[:, 4 * i:4 * i + 4],
-           T.msg[:, o + 2:o + 6], shift(s), None, A.add)
+        for s in sets[i]:
+            o, (at, a, b) = block(s, r) + 2, cols[s]
+            ts(("sc", "beg" if s == r else "m2" if abs(s - r) == 1 else "md"), "pos", T.pos[:, at:at + b - a], T.msg[:, o + a:o + b],
+               shift(s), None, A.add)
 
-    if mid(r):
-        a, z = short(r)
-        ia, iz = src.index(a), src.index(z)
-        if up(r):
-            act(("sc",), "sg", one["sg"], shift(z), F.Sign, scale=-1.0, bias=SH + P - 0.5)
-        else:
-            act(("sc",), "sg", one["sg"], shift(a), F.Sign, bias=-(SH + 0.5))
-        act(("sg",), "ba", one["ba"], one["sg"], scale=(lay[a] - lay["dup"]) / 2.0,
-            bias=(lay[a] + lay["dup"]) / 2.0 - ends(a).start)
-        if iz in later:
-            act(("sg", "b%d" % iz), "bb", one["bb"], one["sg"], F.Relu, scale=-float(WIN))
-        values(ia, ("ba",), one["ba"])
-        if iz in later:
-            act(("bb",), "bb2", one["dv"], one["bb"], scale=-1.0, bias=one["b%d" % iz])
-            values(iz, ("bb2",), one["dv"])
-        side = "2" if up(r) else "1"
-        dma("y", ("c" + side,), "dup", "dup", codes(win[:, lay["dup"]:lay["dup"] + DS]), codes(win[:, lay[a]:lay[a] + DS]))
-        dma("y", ("s" + side,), "dup", "dup", wins[:, lay["dup"]:lay["dup"] + DS], wins[:, lay[a]:lay[a] + DS])
-    else:
+    def marks(*i):
+        a, b = span[i[0]][0], span[i[-1]][1]
+        do("v", V.tensor_copy, ["pos", "tab"] + ["val%d" % k for k in i], "tab", T.tab[:].indirect(T.pos[:, a:b]), T.val[:, 16 * a:16 * b])
+
+    if not mid(r):
         if up(r):
             ts(("sc", "dl"), "dv", one["dv"], shift(r), SH - P - 0.5, one["dl"], A.is_lt, A.mult)
         else:
             ts(("sc", "dl"), "dv", one["dv"], shift(r + 1), SH + 2 * P + 0.5, one["dl"], A.is_gt, A.mult)
-    for i, s in enumerate(src):
-        if abs(s - r) != 1:
-            begins(i)
+    begins(0)
     if not mid(r):
         if up(r):
             ts(("j80", "dv"), "l80", T.l80[:, 0:5], T.j80[:, 0:5], one["dv"], 0.0, A.add, A.max)
         else:
             ts(("j80", "dv"), "l80", T.l80[:, 0:5], T.j80[:, 0:5], one["dv"], float(2 * C - 1), A.add, A.min)
-    for i, s in enumerate(src):
-        if abs(s - r) == 1:
-            begins(i)
 
-    if not mid(r):
+    if mid(r):
+        marks(0)
+        begins(1)
+        marks(1)
+    else:
         side = "1" if up(r) else "2"
-        pick((("l80", "own", "c" + side), ("l80", "own", "s" + side)), "late", T.late[:], T.lates[:],
+        marks(0)
+        begins(1)
+        marks(1)
+        pick((("l80", "xc", "c" + side), ("l80", "xs", "s" + side)), "late", T.late[:], T.lates[:],
              win[:, both], wins[:, both], T.l80[:, 0:5])
         nls += columns([(dr[0], T.late[:], T.lates[:], ("latec", "lates"))])
-
-    do("v", V.tensor_copy, ["pos", "tab0"] + ["val%d" % i for i in range(n)], "tab", T.tab[:].indirect(T.pos[:, 0:4 * n]), T.val[:, 0:64 * n])
     seg = T.tab[:, SH - BACK:SH + P]
     scan(("tab",), "run", T.run[:, 0:P + BACK], seg, seg, 0.0, A.max, A.max)
     scan(("run", "dg"), "held", T.held[:, 0:P], T.dg[:], T.run[:, BACK:BACK + P], 0.0, A.add, A.min)
@@ -441,23 +462,24 @@ def rank_program(g, core, T, topo):
     for h in (0, 1):
         tt(("ya",), "yb", T.yb[:, 16 * h:16 * h + 16], T.ya[:, 0:16], T.ya[:, 16:32], A.max)
     do("v", V.transpose, ("yb",), "yc", T.yc[:], T.yb[:])
-    do("v", V.tensor_copy, ("yc",), "fin", T.fin[:], T.yc[:, 0:16])
+    if mid(r):
+        ts(("yc",), "yc", T.yd[:], T.yc[:, 0:16], WIN - 1, None, A.bitwise_and)
+    do("v", V.tensor_copy, ("yc",), "fin", T.fin[:], T.yd[:] if mid(r) else T.yc[:, 0:16])
 
-    wc = ["fin", "own", "cd"] + [k for k in ("c1", "c2", "dup") if k in ev]
-    wsc = ["fin", "own", "sd"] + [k for k in ("s1", "s2", "dup") if k in ev]
+    wc = ["fin", "xc", "cd"] + [k for k in ("c1", "c2") if k in ev]
+    wsc = ["fin", "xs", "sd"] + [k for k in ("s1", "s2") if k in ev]
     for b in (0, 1):
         pick((wc, wsc), "t%d" % b, T.t2[:, C * b:C * b + C], T.t2s[:, C * b:C * b + C], win[:], wins[:], T.fin[:, 8 * b:8 * b + 8])
-    for b in (0, 1):
-        for o in (0, 1):
+    for o in (0, 1):
+        for b in (0, 1):
             k = 2 * b + o
             do("t", g.tensor.matmul_mx, ("wq", "t%dc" % b, "t%ds" % b), "mm%d" % k, T.ps[:, 512 * k:512 * k + C],
                T.wq[:, C * k:C * k + C], T.ws[:, C * k:C * k + C], T.t2[:, C * b:C * b + C], T.t2s[:, C * b:C * b + C], True, True)
-    for b in (0, 1):
-        lo, hi = slice(C * b, C * b + C), slice(P + C * b, P + C * b + C)
-        do("v", V.tensor_copy, ("mm%d" % (2 * b),), "y0", T.ysb[:, lo], T.ps[:, 1024 * b:1024 * b + C])
-        dma("y", ("y0",), "st", "st", T.y[:, lo], T.ysb[:, lo])
-        act(("mm%d" % (2 * b + 1),), "y1", T.ysb[:, hi], T.ps[:, 1024 * b + 512:1024 * b + 512 + C], F.Copy)
-        dma("s", ("y1",), "st", "st", T.y[:, hi], T.ysb[:, hi])
+    for o in (0, 1):
+        a = P * o
+        do("v", V.tensor_copy, ("mm%d" % o,), "y0", T.ysb[:, a:a + C], T.ps[:, 512 * o:512 * o + C])
+        act(("mm%d" % (2 + o),), "y1", T.ysb[:, a + C:a + P], T.ps[:, 512 * (2 + o):512 * (2 + o) + C], F.Copy)
+        dma("y", ("y0", "y1"), "st", "st", T.y[:, a:a + P], T.ysb[:, a:a + P])
 
     for q, s in own.items():
         ev["end_" + q] = (s, count[q])

@@ -14,12 +14,12 @@ f32, bf, f16, i32, u16, u8, c4 = "float32", "bfloat16", "float16", "int32", "uin
 SCRATCH = {}
 for _n, _w, _d in [
     ("one", 32, f32), ("onei", 8, i32),
-    ("ct", 8, i32), ("cu", 8, u16), ("t8", 8, f32), ("i16", 8, f32), ("k8", 8, f32), ("k8k", 8, f32), ("k8b", 8, bf), ("j16", 8, f32),
-    ("j80", 8, f32), ("i32", 4, f32), ("t32", 4, f32), ("di", 4, f32), ("fl", 4, f32), ("dmp", 4, f32), ("pf", 4, f32),
+    ("ct", 8, i32), ("cu", 8, u16), ("t8", 8, f32), ("i16", 8, f32), ("k8", 8, f32), ("j16", 8, f32),
+    ("i32", 4, f32), ("t32", 4, f32), ("tb", 4, bf), ("di", 4, f32), ("fl", 4, f32), ("dmp", 4, f32), ("pf", 8, f32),
     ("i64", 64, f32), ("t64", 64, f32), ("fm", P, bf), ("dg", P, bf),
-    ("nrow", C, bf), ("nz", C, bf), ("erow", C + 8, f32), ("zrow", C, bf),
-    ("junk", 4 * C, f32), ("acc", 4, f32), ("rm", 4 * C, bf), ("cmp", 4 * C, bf), ("cs", 4 * C, bf), ("comp", 8, u16),
-    ("ce", C, f32), ("cet", C, f32), ("msg", 8 * N, u16), ("tf", 8 * N, f16), ("zer", 8, f32), ("sc", 8, f32),
+    ("nrow", C, bf), ("nz", C, bf), ("zrow", C + 2, bf),
+    ("junk", 8 * C, f32), ("acc", 8, f32), ("cmp", 4 * C, bf), ("cs", 4 * C, f16), ("comp", 8, u16),
+    ("msg", 8 * N, u16), ("tf", 8 * N, f16), ("zer", 8, f32), ("sc", 8, f32),
     ("l80", 6, u16), ("pos", 20, u16), ("val", 5 * 64, f32), ("tab", TAB, f32), ("run", P + 8, f16), ("held", 2 * P, f16),
     ("ya", 32, f16), ("yb", 32, i32), ("yc", 32, i32), ("yd", 16, i32), ("fin", 16, u16),
     ("xb", 512, bf), ("xq", C, c4), ("xs", C, u8), ("xc", C, c4), ("xcs", C, u8),
@@ -29,11 +29,11 @@ for _n, _w, _d in [
     ("r1b", 2, f16), ("r2b", 4, u16), ("rcb", C, c4), ("rsb", C, u8),
 ]:
     SCRATCH[_n] = ("sbuf", [128, _w], _d)
-ONE = {k: i for i, k in enumerate(["paf", "puf", "h16", "paf5", "sum", "mm", "dl", "dv", "b0", "b1", "b2", "b3", "b4"])}
+ONE = {k: i for i, k in enumerate(["paf", "puf", "h16", "paf5", "dl", "dv", "b0", "b1", "b2", "b3", "b4"])}
 ONEI = {k: i for i, k in enumerate(["ip", "ipa", "ipu"])}
 SCRATCH["ps"] = ("psum", [128, 2048], f32)
-SEMAPHORES = ["cl", "xl", "wl", "vs", "ss", "ts", "gs", "ls", "m1", "m2", "md", "cd", "sd",
-              "c1", "s1", "c2", "s2", "r1", "r2", "rc", "rsc", "st"]
+SEMAPHORES = ["cl", "xl", "wl", "vs", "ss", "ts", "gs", "ls", "mt", "m1", "m2", "md", "cd", "sd",
+              "cf", "sf", "r1", "r2", "rc", "rsc", "re", "rse", "st"]
 
 
 def up(r):
@@ -58,8 +58,12 @@ def short(q):
 
 def layout(q):
     out, at = {}, 0
-    if not mid(q) and up(q):
-        at = -DS % 32
+    if not mid(q):
+        if up(q):
+            out = {q - 2: DS + C, q - 1: WIN - REST, q: 2 * WIN - REST - C, q + 1: 2 * WIN + DS}
+        else:
+            out = {q - 1: REST + C, q: WIN + REST, q + 1: 2 * WIN - DS, q + 2: 2 * WIN + REST + 2 * C}
+        return out
     for s in sources(q):
         if mid(q) and s == short(q)[0]:
             at = at + DS if up(q) else WIN - DS
@@ -71,9 +75,13 @@ def layout(q):
     return out
 
 
-def slot(s, q, w):
-    b = layout(q)[s] % WIN
+def slot(s, q, w, skip=0):
+    b = (layout(q)[s] + skip) % WIN
     return slice(b, b + w)
+
+
+def split(r):
+    return r in (1, 2, N - 3, N - 2)
 
 
 def block(s, q):
@@ -92,20 +100,23 @@ def plan(T, topo):
         X = [c for c in relays if topo.die(c) == topo.die(core)]
         Y = [c for c in relays if topo.die(c) != topo.die(core)]
         a, b = (hop[::-1] if up(r) else hop) + far
+        e = r + 2 if up(r) else r - 2
         if far:
-            X, Y = Y, X
-        jobs = {X[0]: [("r1", a), ("r2", a), ("rc", a)], X[1]: [("rsc", a)], Y[0]: [("r1", b)]}
-        if not far:
-            jobs[Y[0]] += [("r2", b), ("rc", b)]
-            jobs[Y[1]] = [("rsc", b)]
-        if mid(r):
-            jobs[X[0]].append(("rc", r + 2 if up(r) else r - 2))
-            jobs[X[1]].append(("rsc", r + 2 if up(r) else r - 2))
+            jobs = {X[0]: [("r1", a), ("r2", a)], X[1]: [("r1", b)], Y[0]: [("rc", a)], Y[1]: [("rsc", a)]}
+        elif split(r):
+            jobs = {X[0]: [(k, a) for k in ("r1", "r2", "re", "rse", "rc")], X[1]: [(k, b) for k in ("r1", "r2", "rc")],
+                    Y[0]: [("rsc", a)], Y[1]: [("rsc", b)]}
+            if mid(r):
+                jobs[X[1]].append(("rc", e))
+                jobs[Y[0]].append(("rsc", e))
+        else:
+            jobs = {X[0]: [("r1", a), ("r2", a), ("rsc", a), ("rsc", e)], X[1]: [("r1", b), ("r2", b), ("rsc", b)],
+                    Y[0]: [("rc", a), ("rc", e)], Y[1]: [("rc", b)]}
         out.append({"direct": direct, "jobs": jobs})
     return out
 
 
-SY = 0
+PARTS = {"r1": 4, "r2": 2, "rc": 2, "rsc": 2, "re": 2, "rse": 2}
 
 
 def mask_of(es):
@@ -145,6 +156,10 @@ def ends(r):
     return slice(REST, C) if up(r) else slice(0, DS)
 
 
+def further(r):
+    return slice(0, REST) if up(r) else slice(DS, C)
+
+
 def relay_program(g, core, T, topo, r, jobs, got):
     send = sender(g, core, T, topo)
     n, seen = 0, set()
@@ -152,19 +167,21 @@ def relay_program(g, core, T, topo, r, jobs, got):
         dst = T.cores[q]
         o = block(r, q)
         win, wins = window(T, q)
-        cut = ends(r) if abs(q - r) == 2 or (mid(q) and short(q)[0] == r) else slice(0, C)
-        side = "d" if abs(q - r) == 2 else "1" if r < q else "2"
+        cut = further(r) if what in ("re", "rse") else ends(r) if abs(q - r) == 2 or split(r) else slice(0, C)
+        side = "f" if what in ("re", "rse") else "d"
+        if what != "r1":
+            at = slot(r, q, cut.stop - cut.start, cut.start if abs(q - r) == 1 and not mid(q) else 0)
         if what not in seen:
-            g.wait_ge(T.sem[what], got)
+            g.wait_ge(T.sem[what], got // PARTS[what])
             seen.add(what)
         if what == "r1":
             item = (T.tf[:, o:o + 1], T.r1b[:, 0:1], "m1")
         elif what == "r2":
             item = (T.msg[:, o + 2:o + 6], T.r2b[:], "m2")
-        elif what == "rc":
-            item = (codes(win[:, slot(r, q, cut.stop - cut.start)]), codes(T.rcb[:, cut]), "c" + side)
+        elif what in ("rc", "re"):
+            item = (codes(win[:, at]), codes(T.rcb[:, cut]), "c" + side)
         else:
-            item = (wins[:, slot(r, q, cut.stop - cut.start)], T.rsb[:, cut], "s" + side)
+            item = (wins[:, at], T.rsb[:, cut], "s" + side)
         n += send([(dst, topo.engines(core, dst)) + item])
     g.wait_ge(T.sem["ls"], n)
 
@@ -175,21 +192,21 @@ def rank_program(g, core, T, topo):
     if r is None:
         for k in range(N):
             if core in pl[k]["jobs"]:
-                relay_program(g, core, T, topo, k, pl[k]["jobs"][core], len(topo.engines(T.cores[k], core)) // 2)
+                relay_program(g, core, T, topo, k, pl[k]["jobs"][core], len(topo.engines(T.cores[k], core)))
         return
     me = pl[r]
     send = sender(g, core, T, topo)
     queues = {"v": g.vector, "s": g.scalar, "t": g.tensor, "g": g, "y": g.sync}
     own = {"v": "vs", "s": "ss", "t": "ts", "g": "gs"}
     count = {"v": 0, "s": 0, "t": 0, "g": 0}
-    ev, seen, final = {}, {}, {}
+    ev, seen, final, made = {}, {}, {}, {}
 
     def need(q, *keys):
         m = {}
         for k in keys:
             s, v = ev[k]
             m[s] = max(m.get(s, 0), v)
-        for s, v in m.items():
+        for s, v in sorted(m.items(), key=lambda x: made.get(x, 0)):
             if seen.get((q, s), 0) < v:
                 queues[q].wait_ge(T.sem[s], v)
                 seen[(q, s)] = v
@@ -199,6 +216,7 @@ def rank_program(g, core, T, topo):
         fn(*a, **kw).then_inc(T.sem[own[q]], 1)
         count[q] += 1
         ev[write] = (own[q], count[q])
+        made[ev[write]] = len(made) + 1
 
     def dma(q, reads, write, sem, out, in_):
         need(q, *reads)
@@ -208,6 +226,7 @@ def rank_program(g, core, T, topo):
 
     V, S = g.vector, g.scalar
     one = {k: T.one[:, i:i + 1] for k, i in ONE.items()}
+    one["sum"], one["mm"] = T.pf[:, 0:1], T.pf[:, 1:2]
     onei = {k: T.onei[:, i:i + 1] for k, i in ONEI.items()}
     src, lay = sources(r), layout(r)
     n = len(src)
@@ -248,14 +267,11 @@ def rank_program(g, core, T, topo):
     iota("i32", [[32, 4]])
     iota("i64", [[32, 4], [1, 16]])
     iota("fm", [[0, 16], [1, 16]])
-    fill("rm1", T.rm[:], 1.0)
     ts(("ip",), "ipa", onei["ipa"], onei["ip"], 15, None, A.bitwise_and)
     ts(("ip",), "ipu", onei["ipu"], onei["ip"], 31, None, A.bitwise_and)
-    fill("er0", T.erow[:, 0:1], 0.0)
+    fill("z0", T.zrow[:, 0:1], 0.0)
     do("v", V.tensor_copy, ("ipa",), "paf", one["paf"], onei["ipa"])
     do("v", V.tensor_copy, ("ipu",), "puf", one["puf"], onei["ipu"])
-    do("v", V.memset, ("rm1",), "rm", T.rm[:, 0:4 * C:C], 0.0)
-    fill("cmp0", T.cmp[:, 0:4 * C:C], 0.0)
     fill("tab", T.tab[:, SH - BACK:SH + P], 0.0)
     fill("zer", T.zer[:], 0.0)
     fill("held0", T.held[:, P + 15:2 * P:16], 0.0)
@@ -263,84 +279,85 @@ def rank_program(g, core, T, topo):
     act(("i16", "paf5"), "k8", T.k8[:], T.i16[:], bias=one["paf5"])
     act(("i32", "puf"), "t32", T.t32[:], T.i32[:], bias=one["puf"])
     act(("i16", "paf"), "j16", T.j16[:], T.i16[:], bias=one["paf"])
-    act(("j16",), "k8b", T.k8b[:], T.j16[:], bias=-float(C if up(r) else 0))
+    act(("t32",), "tb", T.tb[:], T.t32[:], scale=-1.0 if up(r) else 1.0, bias=float(C if up(r) else 0))
     act(("paf", "puf"), "h16", one["h16"], one["paf"], scale=-1.0, bias=one["puf"])
     act(("t32",), "di", T.di[:], T.t32[:], bias=float(DUMP + C * r))
 
     do("v", V.tensor_copy, ("ct",), "cu", T.cu[:], T.ct[:])
     ts(("cu", "t8"), "nz", T.nz[:], T.t8[:].indirect(T.cu[:]), 1.0, None, A.min)
     act(("cu", "t8"), "nrow", T.nrow[:], T.t8[:].indirect(T.cu[:]), F.Copy, accum_out=one["sum"])
-    scan(("nz",), "zrow", T.zrow[:], T.nz[:], T.nz[:], 0.0, A.add, A.max)
+    way = slice(None, None, -1 if up(r) else 1)
+    scan(("nz",), "zrow", T.zrow[:, C:0:-1] if up(r) else T.zrow[:, 1:C + 1], T.nz[:, way], T.nz[:, way], 0.0, A.add, A.max)
     do("v", V.tensor_copy, ("nrow",), "tot", T.tf[:, mo:mo + 1], one["sum"])
-    kcol = T.zrow[:, C - 1:C]
+    kcol = T.zrow[:, 1:2] if up(r) else T.zrow[:, C:C + 1]
 
     dr = me["direct"]
 
     def direct_engines(k):
         return part(topo.engines(core, T.cores[dr[k]]), k, len(dr))
 
-    def to_relays(what, out, in_, upper=False):
+    def to_relays(what, out, in_):
         cs = [c for c, jobs in me["jobs"].items() if what in [k for k, q in jobs]]
-        it = [(c, part(topo.engines(core, c), 1 if upper else 1 - i, 2), out, in_, what) for i, c in enumerate(cs)]
-        return sum(send([x]) for x in it) if upper else send(it)
+        return send([(c, part(topo.engines(core, c), PARTS[what] - 1 - i, PARTS[what]), out, in_, what)
+                     for i, c in enumerate(cs)])
     need("g", "tot")
     nls = to_relays("r1", T.r1b[:, 0:1], T.tf[:, mo:mo + 1])
 
-    thr, tk = T.k8, "k8"
-    if up(r):
-        act(("k8", "zrow"), "k8k", T.k8k[:, 0:4], T.k8[:, 0:4], bias=kcol)
-        thr, tk = T.k8k, "k8k"
-    for c in range(4):
-        act(("zrow", tk), "acc", T.junk[:, C * c:C * c + C - 1], T.zrow[:, 0:C - 1], F.Sign,
-            bias=thr[:, c:c + 1], scale=-1.0, accum_out=T.acc[:, c:c + 1])
-        o, k = T.cmp[:, C * c + 1:C * c + C], T.k8b[:, 4 + c:5 + c]
-        if up(r):
-            ts(("zrow", "k8b"), "cmp", o, T.zrow[:, 0:C - 1], kcol, k, A.subtract, A.is_le)
-        else:
-            ts(("zrow", "k8b"), "cmp", o, T.zrow[:, 0:C - 1], k, None, A.is_le)
-    scan(("cmp", "cmp0", "rm"), "cs", T.cs[:], T.rm[:], T.cmp[:], 0.0, A.mult, A.add)
-    scan(("nrow", "er0"), "erow", T.erow[:, 1:C + 1], T.nrow[:], T.nrow[:], 0.0, A.add, A.max)
-    do("v", V.tensor_copy, ("cs",), "comp1", T.comp[:, 4:8], T.cs[:, C - 1:4 * C:C])
-    ts(("acc",), "comp", T.comp[:, 0:4], T.acc[:], 0.5, (C - 1) / 2.0, A.mult, A.add)
+    row = T.zrow[:, 2:C + 1] if up(r) else T.zrow[:, 1:C]
+    for c in range(8):
+        act(("zrow", "k8"), "acc", T.junk[:, C * c:C * c + C - 1], row, F.Sign,
+            bias=T.k8[:, c:c + 1], scale=1.0 if up(r) else -1.0, accum_out=T.acc[:, c:c + 1])
 
-    act(("erow", "comp"), "ce", T.ce[:], T.erow[:, 0:C].indirect(T.comp[:]), F.Copy)
+    for c in range(4):
+        ts(("zrow", "z0", "tb"), "cmp", T.cmp[:, C * c:C * c + C], T.zrow[:, 1:C + 1] if up(r) else T.zrow[:, 0:C], T.tb[:, c:c + 1], None,
+           A.is_lt if up(r) else A.is_gt)
+    ts(("zrow",), "mu", T.tf[:, mo + 1:mo + 2], kcol, float(DS), None, A.max)
+    need("g", "mu")
+    nls += send([(T.cores[q], direct_engines(k), T.tf[:, block(r, q):block(r, q) + 2], T.tf[:, mo:mo + 2], "mt")
+                 for k, q in enumerate(dr)])
     if up(r):
         ts(("t32", "zrow"), "fl", T.fl[:], T.t32[:], kcol, float(C), A.add, A.is_lt)
     else:
         ts(("t32", "zrow"), "fl", T.fl[:], T.t32[:], kcol, None, A.is_ge)
-    do("v", V.quantize_mx, ("xb",), "xq", T.xq[:], T.xs[:], T.xb[:])
-    tt(("fl", "di"), "dmp", T.dmp[:], T.fl[:], T.di[:], A.mult)
-    do("v", V.tensor_copy, ("nrow",), "tu", T.msg[:, mo:mo + 1], one["sum"])
-    do("v", V.transpose, ("ce",), "cet", T.cet[:], T.ce[:])
-    ts(("zrow",), "mu", T.msg[:, mo + 1:mo + 2], kcol, float(DS), None, A.max)
-    tt(("cet", "dmp"), "pf", T.pf[:], T.cet[:, 0:C:32], T.dmp[:], A.add)
+    for c in range(4):
+        scan(("cmp", "nrow"), "cs", T.cs[:, C * c:C * c + C], T.cmp[:, C * c:C * c + C], T.nrow[:], 0.0, A.mult, A.add)
+        if c == 1:
+            tt(("fl", "di"), "dmp", T.dmp[:], T.fl[:], T.di[:], A.mult)
+    tt(("cs", "dmp"), "pf", T.pf[:, 2:6], T.dmp[:], T.cs[:, C - 1:4 * C:C], A.subtract)
     ts(("zrow",), "mm", one["mm"], kcol, float(DS), None, A.max)
-    do("v", V.tensor_copy, ("pf",), "beg", T.msg[:, mo + 2:mo + 6], T.pf[:])
+    ts(("pf",), "beg", T.msg[:, mo + 2:mo + 6], T.pf[:, 2:6], one["sum"], None, A.add)
+
+    do("v", V.quantize_mx, ("xb",), "xq", T.xq[:], T.xs[:], T.xb[:])
+    ts(("acc",), "comp", T.comp[:], T.acc[:], 0.5, (C - 1) / 2.0, A.mult, A.add)
     mine = (win[:, slot(r, r, C)], wins[:, slot(r, r, C)])
     xc, xcs = (T.xc[:], T.xcs[:]) if mid(r) else mine
     pick((("xq", "comp"), ("xq", "comp")), "x", xc, xcs, T.xq[:], T.xs[:], T.comp[:])
 
     need("g", "beg")
     nls += to_relays("r2", T.r2b[:], T.msg[:, mo + 2:mo + 6])
-    nls += send([(T.cores[q], direct_engines(k), T.msg[:, block(r, q):block(r, q) + 6], T.msg[:, mo:mo + 6], "md")
+    nls += send([(T.cores[q], direct_engines(k), T.msg[:, block(r, q) + 2:block(r, q) + 6], T.msg[:, mo + 2:mo + 6], "md")
                  for k, q in enumerate(dr)])
-    need("g", "xs")
-    nls += to_relays("rsc", T.rsb[:], xcs)
-    need("g", "xc")
-    nls += to_relays("rc", codes(T.rcb[:]), codes(xc))
+    x0 = 0 if mid(r) else slot(r, r, C).start
 
-    def columns(items):
-        tot = 0
-        for i in (0, 1):
-            need("g", *[x[3][i] for x in items])
-            tr = []
-            for k, x in enumerate(items):
-                q = x[0]
-                o = window(T, q)[i][:, slot(r, q, DS)]
-                es = part(topo.engines(core, T.cores[q]), k, len(items))
-                tr.append((T.cores[q], es, o, x[2], "sd") if i else (T.cores[q], es, codes(o), codes(x[1]), "cd"))
-            tot += send(tr)
-        return tot
+    def hand(kind, cut):
+        there = slice(x0 + cut.start, x0 + cut.stop)
+        if "s" in kind:
+            need("g", "xs")
+            return to_relays(kind, T.rsb[:, cut], (T.xcs if mid(r) else wins)[:, there])
+        need("g", "xc")
+        return to_relays(kind, codes(T.rcb[:, cut]), codes((T.xc if mid(r) else win)[:, there]))
+    if split(r):
+        nls += hand("re", further(r)) + hand("rse", further(r))
+    for kind in ("rsc", "rc") if split(r) else ("rc", "rsc"):
+        nls += hand(kind, ends(r) if split(r) else slice(0, C))
+
+    def columns(name, w, skip=0):
+        q = r - 2 if up(r) else r + 2
+        dst, at, (cw, sw) = T.cores[q], slot(r, q, w, skip), window(T, q)
+        need("g", name + "c")
+        tot = send([(dst, topo.engines(core, dst), codes(cw[:, at]), codes(T[name][:, 0:w]), "cd")])
+        need("g", name + "s")
+        return tot + send([(dst, topo.engines(core, dst), sw[:, at], T[name + "s"][:, 0:w], "sd")])
 
     j80 = T.j16[:, 0:5]
     if mid(r):
@@ -349,33 +366,31 @@ def rank_program(g, core, T, topo):
         else:
             ts(("j16", "mm"), "l80", T.l80[:, 0:5], j80, one["mm"], float(DS), A.add, A.subtract)
         pick((("xc", "l80"), ("xs", "l80")), "sp", T.sp[:], T.sps[:], T.xc[:], T.xcs[:], T.l80[:, 0:5])
-        nls += columns([(r - 2 if up(r) else r + 2, T.sp[:], T.sps[:], ("spc", "sps"))])
+        nls += columns("sp", DS)
         pick((("xq", "comp"), ("xq", "comp")), "x", mine[0], mine[1], T.xq[:], T.xs[:], T.comp[:])
     else:
-        nbr = r - 1 if up(r) else r + 1
-        both = slice(lay[min(r, nbr)], lay[min(r, nbr)] + 2 * C)
-        other = REST - DS if up(r) else C + DS
+        both = slice(x0 - x0 % 32, WIN) if up(r) else slice(0, REST + C)
+        other = WIN - DS - both.start if up(r) else 0
         if up(r):
-            act(("mm",), "dl", one["dl"], one["mm"], scale=-1.0, bias=float(2 * C - other))
+            act(("mm",), "dl", one["dl"], one["mm"], scale=-1.0, bias=float(x0 % 32 + C - other))
         else:
-            act(("mm",), "dl", one["dl"], one["mm"], bias=float(-DS - other))
-        act(("j16",), "j80", T.j80[:, 0:5], j80, bias=float(other))
+            act(("mm",), "dl", one["dl"], one["mm"], bias=float(x0 - DS))
 
     ts(("fm", "paf"), "dg", T.dg[:], T.fm[:], one["paf"], BIG, A.is_equal, A.mult)
     act(("i64", "h16"), "t64", T.t64[:], T.i64[:], bias=one["h16"])
     do("v", V.quantize_mx, ("wb",), "wq", T.wq[:], T.ws[:], T.wb[:])
 
-    got = {"m1": 0, "m2": 0, "md": 0, "cd": 0, "sd": 0}
+    got = {"mt": 0, "m1": 0, "m2": 0, "md": 0, "cd": 0, "sd": 0}
     for s in range(N):
         for c, jobs in pl[s]["jobs"].items():
             for what, q in jobs:
                 if q == r:
-                    side = "d" if abs(s - r) == 2 else "1" if s < r else "2"
-                    k = {"r1": "m1", "r2": "m2", "rc": "c" + side, "rsc": "s" + side}[what]
+                    k = {"r1": "m1", "r2": "m2", "rc": "cd", "rsc": "sd", "re": "cf", "rse": "sf"}[what]
                     got[k] = got.get(k, 0) + len(topo.engines(c, core))
         if r in pl[s]["direct"]:
             e = len(topo.engines(T.cores[s], core))
             got["md"] += e // len(pl[s]["direct"])
+            got["mt"] += e // len(pl[s]["direct"])
             if (r > s) != up(s):
                 got["cd"] += e
                 got["sd"] += e
@@ -386,7 +401,7 @@ def rank_program(g, core, T, topo):
     sets.append([s for s in src if s not in sets[0]])
     cols, span, at = {}, [], 0
     for group in sets:
-        a = at = at + at % 2
+        a = at = at + at % 2 * (not mid(r))
         for s in group:
             c = (ends(s).start // 32, ends(s).start // 32 + 3) if abs(s - r) == 2 and (r > s) == up(s) else (0, 4)
             cols[s] = (at,) + c
@@ -403,18 +418,15 @@ def rank_program(g, core, T, topo):
             values(s, (), float(lay[s]))
     for s in src:
         if abs(s - r) == 2 and cols[s][1:] == (0, 4):
-            mu, k = T.msg[:, block(s, r) + 1:block(s, r) + 2], "b%d" % (s > r)
+            mu, k = T.tf[:, block(s, r) + 1:block(s, r) + 2], "b%d" % (s > r)
             if up(s):
-                ts(("md",), k, one[k], mu, float(lay[s] - C), None, A.add)
+                ts(("mt",), k, one[k], mu, float(lay[s] - C), None, A.add)
             else:
-                ts(("md",), k, one[k], mu, -1.0, float(lay[s] + DS), A.mult, A.add)
+                ts(("mt",), k, one[k], mu, -1.0, float(lay[s] + DS), A.mult, A.add)
             values(s, (k,), one[k])
 
     m = len(needs(r))
-    two = sorted(block(s, r) for s in dr if s in needs(r))
-    if two:
-        do("v", V.tensor_copy, ("md",), "tot", T.tf[:, two[0]:two[-1] + 1:32], T.msg[:, two[0]:two[-1] + 1:32])
-    scan(("m1", "tot", "zer"), "sc", T.sc[:, 0:m], T.zer[:, 0:m], T.tf[:, 0:8 * (m - 1) + 1:8],
+    scan(("m1", "mt", "tot", "zer"), "sc", T.sc[:, 0:m], T.zer[:, 0:m], T.tf[:, 0:8 * (m - 1) + 1:8],
          float(SH + (N * up(r) - r) * P), A.add, A.subtract if up(r) else A.add)
 
     def shift(s):
@@ -429,7 +441,7 @@ def rank_program(g, core, T, topo):
 
     def marks(*i):
         a, b = span[i[0]][0], span[i[-1]][1]
-        do("v", V.tensor_copy, ["pos", "tab"] + ["val%d" % k for k in i], "tab", T.tab[:].indirect(T.pos[:, a:b]), T.val[:, 16 * a:16 * b])
+        do("v", V.tensor_copy, ["val%d" % k for k in i] + ["pos", "tab"], "tab", T.tab[:].indirect(T.pos[:, a:b]), T.val[:, 16 * a:16 * b])
 
     if not mid(r):
         if up(r):
@@ -438,23 +450,16 @@ def rank_program(g, core, T, topo):
             ts(("sc", "dl"), "dv", one["dv"], shift(r + 1), SH + 2 * P + 0.5, one["dl"], A.is_gt, A.mult)
     begins(0)
     if not mid(r):
-        if up(r):
-            ts(("j80", "dv"), "l80", T.l80[:, 0:5], T.j80[:, 0:5], one["dv"], 0.0, A.add, A.max)
-        else:
-            ts(("j80", "dv"), "l80", T.l80[:, 0:5], T.j80[:, 0:5], one["dv"], float(2 * C - 1), A.add, A.min)
+        ts(("j16", "dv"), "l80", T.l80[:, 0:5], j80, one["dv"], float(other), A.add, A.add)
 
-    if mid(r):
+    if not mid(r):
         marks(0)
-        begins(1)
-        marks(1)
-    else:
-        side = "1" if up(r) else "2"
-        marks(0)
-        begins(1)
-        marks(1)
-        pick((("l80", "xc", "c" + side), ("l80", "xs", "s" + side)), "late", T.late[:], T.lates[:],
+    begins(1)
+    if not mid(r):
+        pick((("l80", "xc", "cf"), ("l80", "xs", "sf")), "late", T.late[:], T.lates[:],
              win[:, both], wins[:, both], T.l80[:, 0:5])
-        nls += columns([(dr[0], T.late[:], T.lates[:], ("latec", "lates"))])
+        nls += columns("late", DS)
+    marks(*((0, 1) if mid(r) else (1,)))
     seg = T.tab[:, SH - BACK:SH + P]
     scan(("tab",), "run", T.run[:, 0:P + BACK], seg, seg, 0.0, A.max, A.max)
     scan(("run", "dg"), "held", T.held[:, 0:P], T.dg[:], T.run[:, BACK:BACK + P], 0.0, A.add, A.min)
@@ -462,28 +467,28 @@ def rank_program(g, core, T, topo):
     for h in (0, 1):
         tt(("ya",), "yb", T.yb[:, 16 * h:16 * h + 16], T.ya[:, 0:16], T.ya[:, 16:32], A.max)
     do("v", V.transpose, ("yb",), "yc", T.yc[:], T.yb[:])
-    if mid(r):
-        ts(("yc",), "yc", T.yd[:], T.yc[:, 0:16], WIN - 1, None, A.bitwise_and)
-    do("v", V.tensor_copy, ("yc",), "fin", T.fin[:], T.yd[:] if mid(r) else T.yc[:, 0:16])
+    ts(("yc",), "yd", T.yd[:], T.yc[:, 0:16], WIN - 1, None, A.bitwise_and)
+    do("v", V.tensor_copy, ("yd",), "fin", T.fin[:], T.yd[:])
 
-    wc = ["fin", "xc", "cd"] + [k for k in ("c1", "c2") if k in ev]
-    wsc = ["fin", "xs", "sd"] + [k for k in ("s1", "s2") if k in ev]
+    wc, wsc = ("xc", "cd", "fin"), ("xs", "sd", "fin")
     for b in (0, 1):
         pick((wc, wsc), "t%d" % b, T.t2[:, C * b:C * b + C], T.t2s[:, C * b:C * b + C], win[:], wins[:], T.fin[:, 8 * b:8 * b + 8])
-    for o in (0, 1):
-        for b in (0, 1):
+    for b in (0, 1):
+        for o in (0, 1):
             k = 2 * b + o
             do("t", g.tensor.matmul_mx, ("wq", "t%dc" % b, "t%ds" % b), "mm%d" % k, T.ps[:, 512 * k:512 * k + C],
                T.wq[:, C * k:C * k + C], T.ws[:, C * k:C * k + C], T.t2[:, C * b:C * b + C], T.t2s[:, C * b:C * b + C], True, True)
-    for o in (0, 1):
-        a = P * o
-        do("v", V.tensor_copy, ("mm%d" % o,), "y0", T.ysb[:, a:a + C], T.ps[:, 512 * o:512 * o + C])
-        act(("mm%d" % (2 + o),), "y1", T.ysb[:, a + C:a + P], T.ps[:, 512 * (2 + o):512 * (2 + o) + C], F.Copy)
-        dma("y", ("y0", "y1"), "st", "st", T.y[:, a:a + P], T.ysb[:, a:a + P])
+    for b in (0, 1):
+        lo, hi = slice(C * b, C * b + C), slice(P + C * b, P + C * b + C)
+        do("v", V.tensor_copy, ("mm%d" % (2 * b),), "y0", T.ysb[:, lo], T.ps[:, 1024 * b:1024 * b + C])
+        dma("y", ("y0",), "st", "st", T.y[:, lo], T.ysb[:, lo])
+        act(("mm%d" % (2 * b + 1),), "y1", T.ysb[:, hi], T.ps[:, 1024 * b + 512:1024 * b + 512 + C], F.Copy)
+        dma("s" if b else "y", ("y1",), "st", "st", T.y[:, hi], T.ysb[:, hi])
 
     for q, s in own.items():
         ev["end_" + q] = (s, count[q])
     for s, v in final.items():
         ev["end_" + s] = (s, v)
     ev["end_ls"] = ("ls", nls)
-    need("g", *[k for k in ev if k.startswith("end_")], *got)
+    need("g", *got, *[k for k in ev if k.startswith("end_") and k != "end_st"])
+    need("g", "end_st")

from concourse.bass import DstId, RemoteDMATransfer
from concourse.mybir import dt, AluOpType as A, ActivationFunctionType as F

N, C, P, DS = 8, 128, 256, 80
REST = C - DS
WIN = 512
BACK = 5
SH = 4 * P + 16
DUMP = SH + 5 * P + 16
TAB = 2 * DUMP + N * C
BIG = 1.0e6

f32, bf, f16, i32, u16, u8, c4 = "float32", "bfloat16", "float16", "int32", "uint16", "uint8", "float8_e4m3fn_x4"
SCRATCH = {}
for _n, _w, _d in [
    ("one", 32, f32), ("onei", 8, i32),
    ("ct", 8, i32), ("cu", 8, u16), ("t8", 8, f32), ("i16", 8, f32), ("k8", 8, f32), ("j16", 8, f32),
    ("i32", 4, f32), ("t32", 4, f32), ("tb", 4, bf), ("di", 4, f32), ("fl", 4, f32), ("dmp", 4, f32), ("pf", 8, f32),
    ("i64", 64, f32), ("t64", 64, f32), ("fm", P, bf), ("dg", P, bf),
    ("nrow", C, bf), ("nz", C, bf), ("zrow", C + 2, bf),
    ("junk", 8 * C, f32), ("acc", 8, f32), ("cmp", 4 * C, bf), ("cs", 4 * C, f16), ("comp", 8, u16),
    ("msg", 8 * N, u16), ("tf", 8 * N, f16), ("zer", 8, f32), ("sc", 8, f32),
    ("l80", 6, u16), ("pos", 20, u16), ("val", 5 * 64, f32), ("tab", TAB, f32), ("run", P + 8, f16), ("held", 2 * P, f16),
    ("ya", 32, f16), ("yb", 32, i32), ("yc", 32, i32), ("yd", 16, i32), ("fin", 16, u16),
    ("xb", 512, bf), ("xq", C, c4), ("xs", C, u8), ("xc", C, c4), ("xcs", C, u8),
    ("sp", DS, c4), ("sps", DS, u8), ("late", DS, c4), ("lates", DS, u8),
    ("wine", WIN, c4), ("wines", WIN, u8), ("winm", WIN, c4), ("winms", WIN, u8), ("t2", P, c4), ("t2s", P, u8),
    ("wb", 2048, bf), ("wq", 512, c4), ("ws", 512, u8), ("ysb", 512, f32),
    ("r1b", 2, f16), ("r2b", 4, u16), ("rcb", C, c4), ("rsb", C, u8),
]:
    SCRATCH[_n] = ("sbuf", [128, _w], _d)
ONE = {k: i for i, k in enumerate(["paf", "puf", "h16", "paf5", "dl", "dv", "b0", "b1", "b2", "b3", "b4"])}
ONEI = {k: i for i, k in enumerate(["ip", "ipa", "ipu"])}
SCRATCH["ps"] = ("psum", [128, 2048], f32)
SEMAPHORES = ["cl", "xl", "wl", "vs", "ss", "ts", "gs", "ls", "mt", "m1", "m2", "md", "cd", "sd",
              "cf", "sf", "r1", "r2", "rc", "rsc", "re", "rse", "st"]


def up(r):
    return r >= N // 2


def mid(q):
    return 2 <= q < N - 2


def sources(q):
    return list(range(max(0, q - 2), min(N, q + 3)))


def needs(q):
    return range(sources(q)[0], N) if up(q) else range(sources(q)[-1])


def short(q):
    return (q + 1, q + 2) if up(q) else (q - 1, q - 2)


def layout(q):
    out, at = {}, 0
    if not mid(q):
        if up(q):
            out = {q - 2: DS + C, q - 1: WIN - REST, q: 2 * WIN - REST - C, q + 1: 2 * WIN + DS}
        else:
            out = {q - 1: REST + C, q: WIN + REST, q + 1: 2 * WIN - DS, q + 2: 2 * WIN + REST + 2 * C}
        return out
    for s in sources(q):
        if mid(q) and s == short(q)[0]:
            at = at + DS if up(q) else WIN - DS
            out[s] = at
            at = at + WIN - DS if up(q) else WIN + DS
        else:
            out[s] = at
            at += DS if abs(s - q) == 2 else C
    return out


def slot(s, q, w, skip=0):
    b = (layout(q)[s] + skip) % WIN
    return slice(b, b + w)


def split(r):
    return r in (1, 2, N - 3, N - 2)


def block(s, q):
    return 8 * (N - 1 - s if up(q) else s)


def plan(T, topo):
    out = []
    for r in range(N):
        core = T.cores[r]
        near = [q for q in sources(r) if q != r]
        far = [q for q in range(N) if abs(q - r) > 2 and r in needs(q)]
        direct = [q for q in near if topo.may_write(core, T.cores[q])]
        hop = [q for q in near if q not in direct]
        relays = [c for c in topo.cores_of(core) if c != core and all(topo.may_write(c, T.cores[q]) for q in hop + far)]
        X = [c for c in relays if topo.die(c) == topo.die(core)]
        Y = [c for c in relays if topo.die(c) != topo.die(core)]
        a, b = (hop[::-1] if up(r) else hop) + far
        e = r + 2 if up(r) else r - 2
        if far:
            jobs = {X[0]: [("r1", a), ("r2", a)], X[1]: [("r1", b)], Y[0]: [("rc", a)], Y[1]: [("rsc", a)]}
        elif split(r):
            jobs = {X[0]: [(k, a) for k in ("r1", "r2", "re", "rse", "rc")], X[1]: [(k, b) for k in ("r1", "r2", "rc")],
                    Y[0]: [("rsc", a)], Y[1]: [("rsc", b)]}
            if mid(r):
                jobs[X[1]].append(("rc", e))
                jobs[Y[0]].append(("rsc", e))
        else:
            jobs = {X[0]: [("r1", a), ("r2", a), ("rsc", a), ("rsc", e)], X[1]: [("r1", b), ("r2", b), ("rsc", b)],
                    Y[0]: [("rc", a), ("rc", e)], Y[1]: [("rc", b)]}
        out.append({"direct": direct, "jobs": jobs})
    return out


PARTS = {"r1": 4, "r2": 2, "rc": 2, "rsc": 2, "re": 2, "rse": 2}


def mask_of(es):
    return sum(1 << e for e in es)


def part(es, k, n):
    w = len(es) // n
    return es[k * w:k * w + w]


def sender(g, core, T, topo):
    def send(items):
        tr = []
        for dst, es, o, i, rsem in items:
            rid, pid = topo.addr(dst, core)
            tr.append(RemoteDMATransfer(dst_ids=[DstId(rid=rid, pnc=pid)], dma_engine_mask=mask_of(es),
                                        remote_sem=T.sem[rsem], src=i, dst=o))
        g.remote_dma_fused(tr, local_sem=T.sem["ls"])
        return sum(len(es) for _, es, _, _, _ in items)
    return send


def codes(v):
    return v.bitcast(dt.uint8)


def words(v):
    return v.bitcast(dt.uint32)


def window(T, q):
    return (T.winm, T.winms) if mid(q) else (T.wine, T.wines)


def ends(r):
    return slice(REST, C) if up(r) else slice(0, DS)


def further(r):
    return slice(0, REST) if up(r) else slice(DS, C)


def relay_program(g, core, T, topo, r, jobs, got):
    send = sender(g, core, T, topo)
    n, seen = 0, set()
    for what, q in jobs:
        dst = T.cores[q]
        o = block(r, q)
        win, wins = window(T, q)
        cut = further(r) if what in ("re", "rse") else ends(r) if abs(q - r) == 2 or split(r) else slice(0, C)
        side = "f" if what in ("re", "rse") else "d"
        if what != "r1":
            at = slot(r, q, cut.stop - cut.start, cut.start if abs(q - r) == 1 and not mid(q) else 0)
        if what not in seen:
            g.wait_ge(T.sem[what], got // PARTS[what])
            seen.add(what)
        if what == "r1":
            item = (T.tf[:, o:o + 1], T.r1b[:, 0:1], "m1")
        elif what == "r2":
            item = (T.msg[:, o + 2:o + 6], T.r2b[:], "m2")
        elif what in ("rc", "re"):
            item = (codes(win[:, at]), codes(T.rcb[:, cut]), "c" + side)
        else:
            item = (wins[:, at], T.rsb[:, cut], "s" + side)
        n += send([(dst, topo.engines(core, dst)) + item])
    g.wait_ge(T.sem["ls"], n)


def rank_program(g, core, T, topo):
    pl = plan(T, topo)
    r = T.rank_of(core)
    if r is None:
        for k in range(N):
            if core in pl[k]["jobs"]:
                relay_program(g, core, T, topo, k, pl[k]["jobs"][core], len(topo.engines(T.cores[k], core)))
        return
    me = pl[r]
    send = sender(g, core, T, topo)
    queues = {"v": g.vector, "s": g.scalar, "t": g.tensor, "g": g, "y": g.sync}
    own = {"v": "vs", "s": "ss", "t": "ts", "g": "gs"}
    count = {"v": 0, "s": 0, "t": 0, "g": 0}
    ev, seen, final, made = {}, {}, {}, {}

    def need(q, *keys):
        m = {}
        for k in keys:
            s, v = ev[k]
            m[s] = max(m.get(s, 0), v)
        for s, v in sorted(m.items(), key=lambda x: made.get(x, 0)):
            if seen.get((q, s), 0) < v:
                queues[q].wait_ge(T.sem[s], v)
                seen[(q, s)] = v

    def do(q, fn, reads, write, *a, **kw):
        need(q, *reads)
        fn(*a, **kw).then_inc(T.sem[own[q]], 1)
        count[q] += 1
        ev[write] = (own[q], count[q])
        made[ev[write]] = len(made) + 1

    def dma(q, reads, write, sem, out, in_):
        need(q, *reads)
        queues[q].dma_start(out, in_).then_inc(T.sem[sem], 16)
        final[sem] = final.get(sem, 0) + 16
        ev[write] = (sem, final[sem])

    V, S = g.vector, g.scalar
    one = {k: T.one[:, i:i + 1] for k, i in ONE.items()}
    one["sum"], one["mm"] = T.pf[:, 0:1], T.pf[:, 1:2]
    onei = {k: T.onei[:, i:i + 1] for k, i in ONEI.items()}
    src, lay = sources(r), layout(r)
    n = len(src)
    win, wins = window(T, r)
    mo = block(r, r)

    def iota(name, pattern, base_=0):
        do("g", g.iota, (), name, T[name][:], pattern, base_, 0, allow_small_or_imprecise_dtypes=True)

    def act(reads, write, out, in_, func=F.Identity, **kw):
        do("s", S.activation, reads, write, out, in_, func, **kw)

    def ts(reads, write, *a):
        do("v", V.tensor_scalar, reads, write, *a)

    def tt(reads, write, *a):
        do("v", V.tensor_tensor, reads, write, *a)

    def scan(reads, write, *a):
        do("v", V.tensor_tensor_scan, reads, write, *a)

    def fill(write, ap, c):
        do("v", V.memset, (), write, ap, c)

    def pick(reads, name, dst, dsts, from_, froms, off):
        do("v", V.tensor_copy, reads[0], name + "c", words(dst), words(from_).indirect(off))
        act(reads[1], name + "s", dsts, froms.indirect(off), F.Copy)

    for k in range(4):
        for q, j in (("y", 2 * k), ("s", 2 * k + 1)):
            dma(q, (), "ct", "cl", T.ct[16 * j:16 * j + 16, 0:8], T.cnt[:])
    dma("y", (), "xb", "xl", T.xb[:], T.x[:])
    dma("y", (), "wb", "wl", T.wb[:], T.w[:])

    do("g", g.iota, (), "ip", onei["ip"], [[1, 1]], 0, 1)
    iota("t8", [[1, 8]])
    iota("i16", [[16, 8]])
    iota("i32", [[32, 4]])
    iota("i64", [[32, 4], [1, 16]])
    iota("fm", [[0, 16], [1, 16]])
    ts(("ip",), "ipa", onei["ipa"], onei["ip"], 15, None, A.bitwise_and)
    ts(("ip",), "ipu", onei["ipu"], onei["ip"], 31, None, A.bitwise_and)
    fill("z0", T.zrow[:, 0:1], 0.0)
    do("v", V.tensor_copy, ("ipa",), "paf", one["paf"], onei["ipa"])
    do("v", V.tensor_copy, ("ipu",), "puf", one["puf"], onei["ipu"])
    fill("tab", T.tab[:, SH - BACK:SH + P], 0.0)
    fill("zer", T.zer[:], 0.0)
    fill("held0", T.held[:, P + 15:2 * P:16], 0.0)
    act(("paf",), "paf5", one["paf5"], one["paf"], bias=0.5 - (C if up(r) else 0))
    act(("i16", "paf5"), "k8", T.k8[:], T.i16[:], bias=one["paf5"])
    act(("i32", "puf"), "t32", T.t32[:], T.i32[:], bias=one["puf"])
    act(("i16", "paf"), "j16", T.j16[:], T.i16[:], bias=one["paf"])
    act(("t32",), "tb", T.tb[:], T.t32[:], scale=-1.0 if up(r) else 1.0, bias=float(C if up(r) else 0))
    act(("paf", "puf"), "h16", one["h16"], one["paf"], scale=-1.0, bias=one["puf"])
    act(("t32",), "di", T.di[:], T.t32[:], bias=float(DUMP + C * r))

    do("v", V.tensor_copy, ("ct",), "cu", T.cu[:], T.ct[:])
    ts(("cu", "t8"), "nz", T.nz[:], T.t8[:].indirect(T.cu[:]), 1.0, None, A.min)
    act(("cu", "t8"), "nrow", T.nrow[:], T.t8[:].indirect(T.cu[:]), F.Copy, accum_out=one["sum"])
    way = slice(None, None, -1 if up(r) else 1)
    scan(("nz",), "zrow", T.zrow[:, C:0:-1] if up(r) else T.zrow[:, 1:C + 1], T.nz[:, way], T.nz[:, way], 0.0, A.add, A.max)
    do("v", V.tensor_copy, ("nrow",), "tot", T.tf[:, mo:mo + 1], one["sum"])
    kcol = T.zrow[:, 1:2] if up(r) else T.zrow[:, C:C + 1]

    dr = me["direct"]

    def direct_engines(k):
        return part(topo.engines(core, T.cores[dr[k]]), k, len(dr))

    def to_relays(what, out, in_):
        cs = [c for c, jobs in me["jobs"].items() if what in [k for k, q in jobs]]
        return send([(c, part(topo.engines(core, c), PARTS[what] - 1 - i, PARTS[what]), out, in_, what)
                     for i, c in enumerate(cs)])
    need("g", "tot")
    nls = to_relays("r1", T.r1b[:, 0:1], T.tf[:, mo:mo + 1])

    row = T.zrow[:, 2:C + 1] if up(r) else T.zrow[:, 1:C]
    for c in range(8):
        act(("zrow", "k8"), "acc", T.junk[:, C * c:C * c + C - 1], row, F.Sign,
            bias=T.k8[:, c:c + 1], scale=1.0 if up(r) else -1.0, accum_out=T.acc[:, c:c + 1])

    for c in range(4):
        ts(("zrow", "z0", "tb"), "cmp", T.cmp[:, C * c:C * c + C], T.zrow[:, 1:C + 1] if up(r) else T.zrow[:, 0:C], T.tb[:, c:c + 1], None,
           A.is_lt if up(r) else A.is_gt)
    ts(("zrow",), "mu", T.tf[:, mo + 1:mo + 2], kcol, float(DS), None, A.max)
    need("g", "mu")
    nls += send([(T.cores[q], direct_engines(k), T.tf[:, block(r, q):block(r, q) + 2], T.tf[:, mo:mo + 2], "mt")
                 for k, q in enumerate(dr)])
    if up(r):
        ts(("t32", "zrow"), "fl", T.fl[:], T.t32[:], kcol, float(C), A.add, A.is_lt)
    else:
        ts(("t32", "zrow"), "fl", T.fl[:], T.t32[:], kcol, None, A.is_ge)
    for c in range(4):
        scan(("cmp", "nrow"), "cs", T.cs[:, C * c:C * c + C], T.cmp[:, C * c:C * c + C], T.nrow[:], 0.0, A.mult, A.add)
        if c == 1:
            tt(("fl", "di"), "dmp", T.dmp[:], T.fl[:], T.di[:], A.mult)
    tt(("cs", "dmp"), "pf", T.pf[:, 2:6], T.dmp[:], T.cs[:, C - 1:4 * C:C], A.subtract)
    ts(("zrow",), "mm", one["mm"], kcol, float(DS), None, A.max)
    ts(("pf",), "beg", T.msg[:, mo + 2:mo + 6], T.pf[:, 2:6], one["sum"], None, A.add)

    do("v", V.quantize_mx, ("xb",), "xq", T.xq[:], T.xs[:], T.xb[:])
    ts(("acc",), "comp", T.comp[:], T.acc[:], 0.5, (C - 1) / 2.0, A.mult, A.add)
    mine = (win[:, slot(r, r, C)], wins[:, slot(r, r, C)])
    xc, xcs = (T.xc[:], T.xcs[:]) if mid(r) else mine
    pick((("xq", "comp"), ("xq", "comp")), "x", xc, xcs, T.xq[:], T.xs[:], T.comp[:])

    need("g", "beg")
    nls += to_relays("r2", T.r2b[:], T.msg[:, mo + 2:mo + 6])
    nls += send([(T.cores[q], direct_engines(k), T.msg[:, block(r, q) + 2:block(r, q) + 6], T.msg[:, mo + 2:mo + 6], "md")
                 for k, q in enumerate(dr)])
    x0 = 0 if mid(r) else slot(r, r, C).start

    def hand(kind, cut):
        there = slice(x0 + cut.start, x0 + cut.stop)
        if "s" in kind:
            need("g", "xs")
            return to_relays(kind, T.rsb[:, cut], (T.xcs if mid(r) else wins)[:, there])
        need("g", "xc")
        return to_relays(kind, codes(T.rcb[:, cut]), codes((T.xc if mid(r) else win)[:, there]))
    if split(r):
        nls += hand("re", further(r)) + hand("rse", further(r))
    for kind in ("rsc", "rc") if split(r) else ("rc", "rsc"):
        nls += hand(kind, ends(r) if split(r) else slice(0, C))

    def columns(name, w, skip=0):
        q = r - 2 if up(r) else r + 2
        dst, at, (cw, sw) = T.cores[q], slot(r, q, w, skip), window(T, q)
        need("g", name + "c")
        tot = send([(dst, topo.engines(core, dst), codes(cw[:, at]), codes(T[name][:, 0:w]), "cd")])
        need("g", name + "s")
        return tot + send([(dst, topo.engines(core, dst), sw[:, at], T[name + "s"][:, 0:w], "sd")])

    j80 = T.j16[:, 0:5]
    if mid(r):
        if up(r):
            ts(("j16", "mm"), "l80", T.l80[:, 0:5], j80, one["mm"], float(C), A.subtract, A.add)
        else:
            ts(("j16", "mm"), "l80", T.l80[:, 0:5], j80, one["mm"], float(DS), A.add, A.subtract)
        pick((("xc", "l80"), ("xs", "l80")), "sp", T.sp[:], T.sps[:], T.xc[:], T.xcs[:], T.l80[:, 0:5])
        nls += columns("sp", DS)
        pick((("xq", "comp"), ("xq", "comp")), "x", mine[0], mine[1], T.xq[:], T.xs[:], T.comp[:])
    else:
        both = slice(x0 - x0 % 32, WIN) if up(r) else slice(0, REST + C)
        other = WIN - DS - both.start if up(r) else 0
        if up(r):
            act(("mm",), "dl", one["dl"], one["mm"], scale=-1.0, bias=float(x0 % 32 + C - other))
        else:
            act(("mm",), "dl", one["dl"], one["mm"], bias=float(x0 - DS))

    ts(("fm", "paf"), "dg", T.dg[:], T.fm[:], one["paf"], BIG, A.is_equal, A.mult)
    act(("i64", "h16"), "t64", T.t64[:], T.i64[:], bias=one["h16"])
    do("v", V.quantize_mx, ("wb",), "wq", T.wq[:], T.ws[:], T.wb[:])

    got = {"mt": 0, "m1": 0, "m2": 0, "md": 0, "cd": 0, "sd": 0}
    for s in range(N):
        for c, jobs in pl[s]["jobs"].items():
            for what, q in jobs:
                if q == r:
                    k = {"r1": "m1", "r2": "m2", "rc": "cd", "rsc": "sd", "re": "cf", "rse": "sf"}[what]
                    got[k] = got.get(k, 0) + len(topo.engines(c, core))
        if r in pl[s]["direct"]:
            e = len(topo.engines(T.cores[s], core))
            got["md"] += e // len(pl[s]["direct"])
            got["mt"] += e // len(pl[s]["direct"])
            if (r > s) != up(s):
                got["cd"] += e
                got["sd"] += e
    for k, v in got.items():
        ev[k] = (k, v)

    sets = [[s for s in src if abs(s - r) != 1]]
    sets.append([s for s in src if s not in sets[0]])
    cols, span, at = {}, [], 0
    for group in sets:
        a = at = at + at % 2 * (not mid(r))
        for s in group:
            c = (ends(s).start // 32, ends(s).start // 32 + 3) if abs(s - r) == 2 and (r > s) == up(s) else (0, 4)
            cols[s] = (at,) + c
            at += c[1] - c[0]
        span.append((a, at))

    def values(s, reads, bias):
        at, a, b = cols[s]
        act(("t64",) + reads, "val%d" % (s in sets[1]), T.val[:, 16 * at:16 * (at + b - a)], T.t64[:, 16 * a:16 * b], bias=bias)
    for s in sets[1] + sets[0]:
        if (mid(r) and s == short(r)[0]) or cols[s][1:] != (0, 4):
            values(s, (), float(lay[s] - ends(s).start))
        elif abs(s - r) < 2:
            values(s, (), float(lay[s]))
    for s in src:
        if abs(s - r) == 2 and cols[s][1:] == (0, 4):
            mu, k = T.tf[:, block(s, r) + 1:block(s, r) + 2], "b%d" % (s > r)
            if up(s):
                ts(("mt",), k, one[k], mu, float(lay[s] - C), None, A.add)
            else:
                ts(("mt",), k, one[k], mu, -1.0, float(lay[s] + DS), A.mult, A.add)
            values(s, (k,), one[k])

    m = len(needs(r))
    scan(("m1", "mt", "tot", "zer"), "sc", T.sc[:, 0:m], T.zer[:, 0:m], T.tf[:, 0:8 * (m - 1) + 1:8],
         float(SH + (N * up(r) - r) * P), A.add, A.subtract if up(r) else A.add)

    def shift(s):
        j = N - 1 - s if up(r) else s - 1
        return T.sc[:, j:j + 1] if j >= 0 else float(SH - r * P)

    def begins(i):
        for s in sets[i]:
            o, (at, a, b) = block(s, r) + 2, cols[s]
            ts(("sc", "beg" if s == r else "m2" if abs(s - r) == 1 else "md"), "pos", T.pos[:, at:at + b - a], T.msg[:, o + a:o + b],
               shift(s), None, A.add)

    def marks(*i):
        a, b = span[i[0]][0], span[i[-1]][1]
        do("v", V.tensor_copy, ["val%d" % k for k in i] + ["pos", "tab"], "tab", T.tab[:].indirect(T.pos[:, a:b]), T.val[:, 16 * a:16 * b])

    if not mid(r):
        if up(r):
            ts(("sc", "dl"), "dv", one["dv"], shift(r), SH - P - 0.5, one["dl"], A.is_lt, A.mult)
        else:
            ts(("sc", "dl"), "dv", one["dv"], shift(r + 1), SH + 2 * P + 0.5, one["dl"], A.is_gt, A.mult)
    begins(0)
    if not mid(r):
        ts(("j16", "dv"), "l80", T.l80[:, 0:5], j80, one["dv"], float(other), A.add, A.add)

    if not mid(r):
        marks(0)
    begins(1)
    if not mid(r):
        pick((("l80", "xc", "cf"), ("l80", "xs", "sf")), "late", T.late[:], T.lates[:],
             win[:, both], wins[:, both], T.l80[:, 0:5])
        nls += columns("late", DS)
    marks(*((0, 1) if mid(r) else (1,)))
    seg = T.tab[:, SH - BACK:SH + P]
    scan(("tab",), "run", T.run[:, 0:P + BACK], seg, seg, 0.0, A.max, A.max)
    scan(("run", "dg"), "held", T.held[:, 0:P], T.dg[:], T.run[:, BACK:BACK + P], 0.0, A.add, A.min)
    do("v", V.transpose, ("held", "held0"), "ya", T.ya[:], T.held[:, 15:2 * P:16])
    for h in (0, 1):
        tt(("ya",), "yb", T.yb[:, 16 * h:16 * h + 16], T.ya[:, 0:16], T.ya[:, 16:32], A.max)
    do("v", V.transpose, ("yb",), "yc", T.yc[:], T.yb[:])
    ts(("yc",), "yd", T.yd[:], T.yc[:, 0:16], WIN - 1, None, A.bitwise_and)
    do("v", V.tensor_copy, ("yd",), "fin", T.fin[:], T.yd[:])

    wc, wsc = ("xc", "cd", "fin"), ("xs", "sd", "fin")
    for b in (0, 1):
        pick((wc, wsc), "t%d" % b, T.t2[:, C * b:C * b + C], T.t2s[:, C * b:C * b + C], win[:], wins[:], T.fin[:, 8 * b:8 * b + 8])
    for b in (0, 1):
        for o in (0, 1):
            k = 2 * b + o
            do("t", g.tensor.matmul_mx, ("wq", "t%dc" % b, "t%ds" % b), "mm%d" % k, T.ps[:, 512 * k:512 * k + C],
               T.wq[:, C * k:C * k + C], T.ws[:, C * k:C * k + C], T.t2[:, C * b:C * b + C], T.t2s[:, C * b:C * b + C], True, True)
    for b in (0, 1):
        lo, hi = slice(C * b, C * b + C), slice(P + C * b, P + C * b + C)
        do("v", V.tensor_copy, ("mm%d" % (2 * b),), "y0", T.ysb[:, lo], T.ps[:, 1024 * b:1024 * b + C])
        dma("y", ("y0",), "st", "st", T.y[:, lo], T.ysb[:, lo])
        act(("mm%d" % (2 * b + 1),), "y1", T.ysb[:, hi], T.ps[:, 1024 * b + 512:1024 * b + 512 + C], F.Copy)
        dma("s" if b else "y", ("y1",), "st", "st", T.y[:, hi], T.ysb[:, hi])

    for q, s in own.items():
        ev["end_" + q] = (s, count[q])
    for s, v in final.items():
        ev["end_" + s] = (s, v)
    ev["end_ls"] = ("ls", nls)
    need("g", *got, *[k for k in ev if k.startswith("end_") and k != "end_st"])
    need("g", "end_st")
